import numpy as np
import ml_dtypes


def mxq(x, axis, fmt="e4m3"):
    dtype, down = {"e4m3": (ml_dtypes.float8_e4m3fn, 7), "e5m2": (ml_dtypes.float8_e5m2, 14)}[fmt]
    v = np.moveaxis(np.asarray(x, np.float32).astype(ml_dtypes.bfloat16).astype(np.float64), axis, -1)
    blocks = v.reshape(v.shape[:-1] + (-1, 32))
    amax = np.abs(blocks).max(-1, keepdims=True)
    byte = np.maximum(np.where(amax > 0, np.frexp(amax)[1] - 1 + 127, 0) - down, 1)
    scale = np.exp2(byte - 127.0)
    codes = (blocks / scale).astype(np.float32).astype(dtype).astype(np.float64)
    return np.moveaxis((codes * scale).reshape(v.shape), -1, axis)


WIDE = False


def mx_kscale(k):
    if not WIDE:
        return np.ones(k)
    levels = np.array([10, -10, 5, -5, 0])
    if k % 512:
        return np.exp2(np.random.permutation(np.resize(levels, k // 32))).repeat(32)
    a = np.empty((k // 512, 16))
    for p in range(k // 512):
        a[p, :8] = np.random.permutation(np.resize(levels, 8))
        for g in range(8):
            far = levels[np.abs(levels - a[p, g]) >= 10]
            a[p, g + 8] = far[np.random.randint(len(far))]
    return np.exp2(a.ravel()).repeat(32)


BF16 = ml_dtypes.bfloat16


def bf(x):
    return np.asarray(x, np.float32).astype(BF16)


def f64(x):
    return np.asarray(x).astype(np.float64)


E2M1 = np.array([0.0, 0.5, 1.0, 1.5, 2.0, 3.0, 4.0, 6.0, -0.0, -0.5, -1.0, -1.5, -2.0, -3.0, -4.0, -6.0])


def pack_weight(w, fmt):
    k, n = w.shape
    w = f64(bf(w)).reshape(k // 32, 32, n)
    amax = np.abs(w).max(1)
    if fmt == "e4m3":
        byte = np.frexp(amax)[1] - 1 + 127 - 7
    else:
        mant, ex = np.frexp(amax / 6.0)
        byte = np.where(mant > 0.5, ex, ex - 1) + 127
    byte = np.clip(np.where(amax > 0, byte, 1), 1, 254)
    scaled = (w * np.exp2(127.0 - byte)[:, None, :]).reshape(k, n).astype(np.float32)
    by_word = np.ascontiguousarray(scaled.reshape(k // 512, 128, 4, n).transpose(0, 1, 3, 2))
    if fmt == "e4m3":
        words = by_word.astype(ml_dtypes.float8_e4m3fn).view(np.uint8)
    else:
        c = by_word.astype(ml_dtypes.float4_e2m1fn).view(np.uint8) & 0xF
        words = c[..., 0::2] | (c[..., 1::2] << 4)
    return np.ascontiguousarray(words), np.ascontiguousarray(byte.astype(np.uint8).reshape(k // 512, 16, n))


def unpack_weight(words, scales, fmt):
    g, p, n, _ = words.shape
    if fmt == "e4m3":
        vals = np.ascontiguousarray(words).view(ml_dtypes.float8_e4m3fn).astype(np.float64)
    else:
        nib = np.empty((g, p, n, 4), np.uint8)
        nib[..., 0::2] = words & 0xF
        nib[..., 1::2] = words >> 4
        vals = E2M1[nib]
    vals = vals * np.repeat(np.exp2(scales.astype(np.float64) - 127.0), 8, axis=1)[..., None]
    return vals.transpose(0, 1, 3, 2).reshape(g * 512, n)
def pack4(w):
    words, scales = pack_weight(w, "e2m1")
    return words.reshape(words.shape[0], 128, -1), scales


def unpack4(words, scales):
    return unpack_weight(words.reshape(words.shape[0], 128, -1, 2), scales, "e2m1")


E4M3FN = np.array([(-1.0 if i & 128 else 1.0) * ((1.0 + (i & 7) / 8.0) * 2.0 ** (((i >> 3) & 15) - 7) if i & 120 else (i & 7) * 2.0 ** -9) for i in range(256)])


def e4m3fn_bytes(y):
    return np.clip(np.asarray(y, np.float64), -448.0, 448.0).astype(np.float32).astype(ml_dtypes.float8_e4m3fn).view(np.uint8)


def e4m3fn_values(b):
    return E4M3FN[b]


H, W, D, F = 2, 1024, 512, 512
P = 2
L = W + W // P
DISP_STEP = 128.0
WIDTH0 = 128.0
WIDTH1 = 256.0


def scanline_correlation(f_left, f_right):
    d = f_left.shape[-1]
    prod = mxq(f_left, 2, "e4m3") @ mxq(f_right, 2, "e4m3").transpose(0, 2, 1)
    return prod / np.sqrt(d)


def pool_pairs(corr):
    h, w, n = corr.shape
    return np.mean(corr.reshape(h, w, n // P, P), axis=-1)


def gaussian_window(pos, ctr, width):
    t = (pos[None, None, :] - ctr[:, :, None]) / width
    return np.exp(-0.5 * t ** 2)


def draw0():
    s, t = mx_kscale(D), mx_kscale(L)
    f_left = bf(np.random.standard_normal((H, W, D)) * s)
    f_right = bf(np.random.standard_normal((H, W, D)) / s)
    disp = bf(np.random.uniform(0.0, 2.0, (H, W)))
    gain = bf((1.0 + 0.1 * np.random.standard_normal(L)) * t)
    words, scales = pack4(np.random.standard_normal((L, F)) * 3.135 / np.sqrt(L) / t[:, None])
    return {
        "f_left": f_left,
        "f_right": f_right,
        "disp": disp,
        "gain": gain,
        "w_corr_words": words,
        "w_corr_scales": scales,
        "w_disp": bf(np.random.standard_normal(F)),
        "b_mot": bf(np.random.standard_normal(F) * 0.3),
    }


def core(f_left, f_right, disp, gain, w_corr_words, w_corr_scales, w_disp, b_mot):
    f_left, f_right, disp, gain = f64(f_left), f64(f_right), f64(disp), f64(gain)
    w_disp, b_mot = f64(w_disp), f64(b_mot)
    w = f_left.shape[1]

    corr = scanline_correlation(f_left, f_right)

    half = pool_pairs(corr)

    i = np.arange(w, dtype=np.float64)
    ctr = i[None, :] - DISP_STEP * disp

    j0 = np.arange(w, dtype=np.float64)
    j1 = np.arange(w // P, dtype=np.float64)
    win0 = gaussian_window(j0, ctr, WIDTH0)
    win1 = gaussian_window(2.0 * j1 + 0.5, ctr, WIDTH1)

    c = np.concatenate([win0 * corr, win1 * half], axis=-1)

    cg = c * gain

    pre = (mxq(cg, 2, "e4m3") @ unpack4(w_corr_words, w_corr_scales)) + (disp - 1.0)[..., None] * w_disp + b_mot
    return np.maximum(pre, 0.0)


def setup_inputs():
    drawn = draw0()
    full = np.asarray(drawn['f_right']).astype(np.float64)
    scale = (np.abs(full).reshape(2, 8, 128, 4, 128).max(axis=(2, 4)) / 448.0).astype(np.float32)
    given = {}
    for key, value in drawn.items():
        if key == 'f_right':
            given['f_right_bytes'] = e4m3fn_bytes(full / np.repeat(np.repeat(scale.astype(np.float64), 128, axis=1), 128, axis=2))
            given['f_right_scale'] = scale
        else:
            given[key] = value
    return given


def reference(f_left, f_right_bytes, f_right_scale, disp, gain, w_corr_words, w_corr_scales, w_disp, b_mot):
    return core(f_left, e4m3fn_values(f_right_bytes) * np.repeat(np.repeat(f_right_scale.astype(np.float64), 128, axis=1), 128, axis=2), disp, gain, w_corr_words, w_corr_scales, w_disp, b_mot)

@@ -1,0 +1,568 @@
+import math
+from contextlib import ExitStack
+
+import concourse.mybir as mybir
+from concourse.masks import make_identity
+
+H, W, D, F = 2, 1024, 512, 512
+L = W + W // 2
+FLOPS = 2 * H * W * W * D + 2 * H * W * L * F
+
+F32 = mybir.dt.float32
+BF16 = mybir.dt.bfloat16
+I32 = mybir.dt.int32
+U32 = mybir.dt.uint32
+U8 = mybir.dt.uint8
+FP8 = mybir.dt.float8_e4m3fn
+FP8X4 = mybir.dt.float8_e4m3fn_x4
+FP4X4 = mybir.dt.float4_e2m1fn_x4
+ALU = mybir.AluOpType
+ACT = mybir.ActivationFunctionType
+
+P = 128
+NT = 8
+TILES = H * NT
+TERMS = 16
+BIAS_G = range(15)
+RELU_V = ()
+RELU_G = ()
+WIDEN_S0 = 0
+WIDEN_S1 = 0
+PERM = False
+
+
+def tile_stereocorrpyramidmotionencoder_d2p_kernel(
+    tc, f_left, f_right_bytes, f_right_scale, disp, gain, w_corr_words, w_corr_scales, w_disp, b_mot, out
+):
+    nc = tc.nc
+    with ExitStack() as ctx:
+        keep = ctx.enter_context(tc.tile_pool(name="keep", bufs=1))
+        work = ctx.enter_context(tc.tile_pool(name="work", bufs=2))
+        psum = ctx.enter_context(tc.psum_pool(name="psum", bufs=1))
+        ctx.enter_context(tc.manual_schedule())
+
+        def kept(name, shape, dtype):
+            return keep.tile(shape, dtype, name=name, align_bytes=64)
+
+        scale_all = kept("scale_all", [P, H * 8 * 4], F32)
+        gain_rows = kept("gain_rows", [P, 8], BF16)
+        gain_k = kept("gain_k", [P, 3, 4], BF16)
+        disp_i = kept("disp_i", [P, H, NT], BF16)
+        right_bytes = [kept("right_bytes%d" % y, [P, 8, D], U8) for y in range(H)]
+        left = [kept("left%d" % y, [P, NT, D], BF16) for y in range(H)]
+        wd_row = kept("wd_row", [P, F], BF16)
+        b_row = kept("b_row", [P, F], BF16)
+        w_words = kept("w_words", [P, 3, 2 * F], U8)
+        w_scales = kept("w_scales", [P, 3, F], U8)
+
+        nc.scalar.dma_start(out=scale_all[:], in_=f_right_scale.rearrange("y j d -> (y j d)").partition_broadcast(P))
+        nc.scalar.dma_start(out=gain_rows[:], in_=gain[0:W].rearrange("(m s) -> m s", s=8))
+        nc.scalar.dma_start(out=gain_k[:], in_=gain.rearrange("(g p t) -> p g t", p=P, t=4))
+        nc.scalar.dma_start(out=disp_i[:], in_=disp.rearrange("y (q n) -> q y n", n=NT))
+
+        def load_right(y, h):
+            src = f_right_bytes[y].rearrange("(m a b c) d -> m a b (c d)", a=2, b=2, c=2)
+            dst = right_bytes[y][:].rearrange("m (a b c) d -> m a b (c d)", a=2, b=2)
+            nc.sync.dma_start(out=dst[:, :, h, :], in_=src[:, :, h, :])
+
+        def load_left(y, n0, n1):
+            src = f_left[y].rearrange("(q n) d -> q n d", n=NT)
+            nc.sync.dma_start(out=left[y][:, n0:n1, :], in_=src[:, n0:n1, :])
+
+        nc.vector.memset(w_scales[:].rearrange("p g n -> p (g n)").bitcast(I32), 0)
+        load_right(0, 0)
+        load_right(0, 1)
+        load_left(0, 0, 2)
+        load_left(0, 2, 4)
+        load_left(0, 4, 6)
+        load_right(1, 0)
+        for quad in range(4):
+            nc.sync.dma_start(
+                out=w_scales[32 * quad : 32 * quad + 4, :, :].bitcast(I32),
+                in_=w_corr_scales[:, 4 * quad : 4 * quad + 4, :].rearrange("g r n -> r g n").bitcast(I32),
+            )
+        nc.sync.dma_start(out=w_words[:].bitcast(I32), in_=w_corr_words.rearrange("g p n -> p g n").bitcast(I32))
+        nc.sync.dma_start(out=wd_row[:], in_=w_disp.partition_broadcast(P))
+        nc.sync.dma_start(out=b_row[:], in_=b_mot.partition_broadcast(P))
+        load_right(1, 1)
+        load_left(0, 6, 8)
+        load_left(1, 0, 4)
+        load_left(1, 4, 8)
+
+        def counted(name, pattern, base, step):
+            t = kept(name, [P] + [n for (s, n) in pattern], F32)
+            nc.gpsimd.iota(t[:], pattern, base=base, channel_multiplier=step, allow_small_or_imprecise_dtypes=True)
+            return t
+
+        ident32 = kept("ident32", [P, P], F32)
+        make_identity(nc, ident32[:])
+        c_int = counted("c_int", [[0, H], [1, NT]], -512, 8)
+        j_int = counted("j_int", [[512, 2], [1, 4]], -512, 4)
+        ident16 = kept("ident16", [P, P], BF16)
+        c_flat = c_int[:].rearrange("p y n -> p (y n)")
+        j_flat = j_int[:].rearrange("p g t -> p (g t)")
+        c_high = c_flat[:, 0:1]
+
+        col_terms = kept("col_terms", [P, TILES * TERMS + P - TERMS], BF16)
+        row_terms = kept("row_terms", [P, 8, P], BF16)
+        col_v = col_terms[:, 0 : TILES * TERMS].rearrange("p (x k) -> p x k", k=TERMS)
+        row_v = row_terms[:].rearrange("p (g t) k -> p g t k", t=4)
+        pick = kept("pick", [P, 8], F32)
+        half_j2 = kept("half_j2", [P, 8], F32)
+        pos_bias = kept("pos_bias", [P, 4], F32)
+        nc.vector.memset(col_terms[:], 0.0)
+        nc.vector.memset(row_terms[:], 0.0)
+        nc.vector.tensor_reduce(pick[:], ident32[:].rearrange("p (j r) -> p j r", r=16), axis=mybir.AxisListType.X, op=ALU.add)
+        nc.vector.memset(row_terms[:, :, 6:9], 1.0)
+        nc.vector.tensor_copy(out=ident16[:], in_=ident32[:])
+        nc.vector.tensor_copy(out=col_v[:, :, 0:6:3], in_=c_high.unsqueeze(2).to_broadcast([P, TILES, 2]))
+        nc.vector.tensor_scalar(col_v[:, :, 1:6:3], c_flat.unsqueeze(2).to_broadcast([P, TILES, 2]), c_high, None, op0=ALU.subtract)
+        for g in range(2):
+            nc.vector.tensor_copy(out=row_v[:, g, :, 0:3], in_=j_int[:, g, 0:1].unsqueeze(2).to_broadcast([P, 4, 3]))
+            nc.vector.tensor_scalar(
+                row_v[:, g, :, 3:6], c_flat[:, 0:4].unsqueeze(2).to_broadcast([P, 4, 3]), c_high, None, op0=ALU.subtract
+            )
+        nc.vector.scalar_tensor_tensor(half_j2[:], j_flat, -0.5, j_flat, op0=ALU.mult, op1=ALU.mult)
+        nc.vector.tensor_scalar(pos_bias[:], j_int[:, 1, :], 1.0 / 128.0, (0.5 - 512.0) / 256.0, op0=ALU.mult, op1=ALU.add)
+
+        picked = kept("picked", [P, H, 4, 8], F32)
+        scale_m = kept("scale_m", [P, H * 4], F32)
+        sign_rows = kept("sign_rows", [P, 8], F32)
+        sign_pool = kept("sign_pool", [P, 4], F32)
+        scale_signed = kept("scale_signed", [P, H, 8, 4], F32)
+        resign = kept("resign", [P, 4, 2], F32)
+        gain_abs = kept("gain_abs", [P, 12], F32)
+        factors = kept("factors", [P, 3, 12], F32)
+        logs = kept("logs", [P, 3, 12], F32)
+        log_gain = kept("log_gain", [P, 12], F32)
+        log_part = kept("log_part", [P, 12], F32)
+        disp_c = kept("disp_c", [P, TILES], F32)
+        disp_m1 = kept("disp_m1", [P, TILES], F32)
+        centre = kept("centre", [P, TILES], F32)
+        whole = kept("whole", [P, TILES + 8], F32)
+        rest1 = kept("rest1", [P, TILES + 8], F32)
+        rest2 = kept("rest2", [P, TILES + 8], F32)
+        pieces = kept("pieces", [P, 3, TILES + 8], BF16)
+        gain_flat = gain_k[:].rearrange("p g t -> p (g t)")
+        disp_flat = disp_i[:].rearrange("p y n -> p (y n)")
+
+        small = [
+            lambda: nc.vector.tensor_tensor(
+                picked[:],
+                scale_all[:].rearrange("p (y j d) -> p y d j", y=H, d=4),
+                pick[:].unsqueeze(1).unsqueeze(1).to_broadcast([P, H, 4, 8]),
+                op=ALU.mult,
+            ),
+            lambda: nc.vector.tensor_scalar(sign_rows[:], gain_rows[:], 0.0, 0.5, op0=ALU.is_ge, op1=ALU.subtract),
+            lambda: nc.vector.tensor_reduce(
+                scale_m[:], picked[:].rearrange("p y d j -> p (y d) j"), axis=mybir.AxisListType.X, op=ALU.add
+            ),
+            lambda: nc.vector.scalar_tensor_tensor(gain_abs[:], gain_flat, -1.0, gain_flat, op0=ALU.mult, op1=ALU.max),
+            lambda: nc.vector.scalar_tensor_tensor(
+                scale_signed[:, 0, :, :],
+                scale_m[:, 0:4].unsqueeze(1).to_broadcast([P, 8, 4]),
+                2.0,
+                sign_rows[:].unsqueeze(2).to_broadcast([P, 8, 4]),
+                op0=ALU.mult,
+                op1=ALU.mult,
+            ),
+            lambda: nc.vector.tensor_scalar(factors[:, 0, :], gain_abs[:], 2.0**-64, 2.0**64, op0=ALU.max, op1=ALU.min),
+            lambda: nc.vector.tensor_scalar(factors[:, 1, :], gain_abs[:], 2.0**-64, 1.0, op0=ALU.mult, op1=ALU.max),
+            lambda: nc.vector.tensor_scalar(log_part[:], gain_abs[:], 2.0**-64, 2.0**64, op0=ALU.min, op1=ALU.mult),
+            lambda: nc.vector.tensor_scalar(sign_pool[:], gain_k[:, 2, :], 0.0, 0.5, op0=ALU.is_ge, op1=ALU.subtract),
+            lambda: nc.vector.tensor_scalar(factors[:, 2, :], log_part[:], 2.0**-64, None, op0=ALU.max),
+        ]
+        for step in small:
+            step()
+        nc.scalar.activation(out=logs[:], in_=factors[:], func=ACT.Ln)
+        one = kept("one", [P, 1], F32)
+        nc.scalar.activation(out=one[:], in_=logs[:, 0, 0:1], func=ACT.Exp, scale=0.0)
+
+        small = [
+            lambda: nc.vector.scalar_tensor_tensor(
+                resign[:],
+                sign_rows[:].rearrange("p (t e) -> p t e", e=2),
+                4.0,
+                sign_pool[:].unsqueeze(2).to_broadcast([P, 4, 2]),
+                op0=ALU.mult,
+                op1=ALU.mult,
+            ),
+            lambda: nc.vector.tensor_scalar(disp_c[:], disp_flat, 1024.0, -1024.0, op0=ALU.min, op1=ALU.max),
+            lambda: nc.vector.tensor_reduce(
+                log_gain[:], logs[:].rearrange("p r k -> p k r"), axis=mybir.AxisListType.X, op=ALU.add
+            ),
+            lambda: nc.vector.scalar_tensor_tensor(
+                centre[:], disp_c[:], -128.0, c_flat, op0=ALU.mult, op1=ALU.add
+            ),
+            lambda: nc.vector.scalar_tensor_tensor(
+                whole[:, TILES:], log_gain[:, 0:8], 16384.0, half_j2[:], op0=ALU.mult, op1=ALU.add
+            ),
+            lambda: nc.vector.scalar_tensor_tensor(whole[:, 0:TILES], centre[:], -0.5, centre[:], op0=ALU.mult, op1=ALU.mult),
+            lambda: nc.vector.tensor_scalar(
+                col_v[:, :, 2:6:3], disp_c[:].unsqueeze(2).to_broadcast([P, TILES, 2]), -128.0, None, op0=ALU.mult
+            ),
+            lambda: nc.vector.tensor_copy(out=pieces[:, 0, :], in_=whole[:]),
+            lambda: nc.vector.tensor_tensor(rest1[:], whole[:], pieces[:, 0, :], op=ALU.subtract),
+            lambda: nc.vector.tensor_copy(out=pieces[:, 1, :], in_=rest1[:]),
+            lambda: nc.vector.tensor_tensor(rest2[:], rest1[:], pieces[:, 1, :], op=ALU.subtract),
+            lambda: nc.vector.tensor_copy(out=pieces[:, 2, :], in_=rest2[:]),
+            lambda: nc.vector.tensor_copy(out=col_v[:, :, 6:9], in_=pieces[:, :, 0:TILES].rearrange("p r x -> p x r")),
+            lambda: nc.vector.tensor_copy(out=row_terms[:, :, 9:12], in_=pieces[:, :, TILES:].rearrange("p r x -> p x r")),
+            lambda: nc.vector.tensor_copy(out=col_v[:, :, 9:12], in_=one[:].unsqueeze(2).to_broadcast([P, TILES, 3])),
+            lambda: nc.vector.tensor_scalar(disp_m1[:], disp_flat, 1.0, None, op0=ALU.subtract),
+            lambda: nc.vector.scalar_tensor_tensor(
+                scale_signed[:, 1, :, :],
+                scale_m[:, 4:8].unsqueeze(1).to_broadcast([P, 8, 4]),
+                2.0,
+                sign_rows[:].unsqueeze(2).to_broadcast([P, 8, 4]),
+                op0=ALU.mult,
+                op1=ALU.mult,
+            ),
+        ]
+
+        right0 = kept("right0", [P, 8, D], BF16)
+        right1 = kept("right1", [P, 8, D], BF16)
+        r_codes = [[kept("r_codes%d%d" % (y, v), [P, 4, 256], U32) for v in range(2)] for y in range(H)]
+        r_scales = [[kept("r_scales%d%d" % (y, v), [P, 4, 256], U8) for v in range(2)] for y in range(H)]
+        l_codes = [kept("l_codes%d" % y, [P, W], U32) for y in range(H)]
+        l_scales = [kept("l_scales%d" % y, [P, W], U8) for y in range(H)]
+        moving = kept("moving", [P, TILES, P], BF16)
+        stationary = kept("stationary", [P, 8, P], BF16)
+        live = {}
+        turns = []
+
+        def widen(y, s, block, on_scalar):
+            cols = slice(block * P, (block + 1) * P)
+            src = right_bytes[y][:, s, cols].bitcast(FP8)
+            factor = scale_signed[:, y, s, block : block + 1]
+            if on_scalar:
+                nc.scalar.activation(out=right0[:, s, cols], in_=src, func=ACT.Copy, scale=factor)
+            elif PERM:
+                dst = right0[:, s, :].rearrange("p (u w e) -> p w u e", u=2, e=2)[:, block * 32 : (block + 1) * 32, :, :]
+                nc.vector.tensor_scalar(dst, src.rearrange("p (w u e) -> p w u e", u=2, e=2), factor, None, op0=ALU.mult)
+            else:
+                nc.vector.tensor_scalar(right0[:, s, cols], src, factor, None, op0=ALU.mult)
+
+        def flip(s):
+            nc.vector.tensor_scalar(right1[:, s, :], right0[:, s, :], resign[:, s // 2, s % 2 : s % 2 + 1], None, op0=ALU.mult)
+
+        def turn_bank(dtype, tags):
+            tag = tags[len(turns) % len(tags)]
+            turns.append(tag)
+            return psum.tile([P, 512 if dtype == F32 else 1024], dtype, name=tag, tag=tag)
+
+        def turn(key, rows_a, rows_b, tags=("turn0", "turn1")):
+            bank = turn_bank(F32, tags)
+            for a, rows in enumerate((rows_a, rows_b)):
+                words = rows.bitcast(F32)
+                for u in range(2):
+                    src = words[:, u * P : (u + 1) * P] if (PERM and key[0] == "r") else words[:, u : 256 : 2]
+                    nc.tensor.transpose(bank[:, (2 * a + u) * P : (2 * a + u + 1) * P], src, ident32[:])
+            live[key] = bank
+
+        def empty(key, weave, on_vector=False):
+            grouped = work.tile([P, 512], F32, name="grouped", bufs=6, align_bytes=64)
+            if weave:
+                src = live[key][:].rearrange("p (a r) -> p r a", a=4)
+                dst = grouped[:].rearrange("p (r a) -> p r a", a=4)
+            else:
+                src = live[key][:].rearrange("p (e u r) -> p e r u", e=2, u=2)
+                dst = grouped[:].rearrange("p (e r u) -> p e r u", e=2, u=2)
+            if on_vector:
+                nc.vector.tensor_copy(out=dst, in_=src)
+            else:
+                nc.scalar.copy(out=dst, in_=src)
+            live[key] = grouped
+
+        def quantise(key, codes, scales):
+            nc.vector.quantize_mx(out=codes.bitcast(FP8X4), scales=scales, in_=live[key][:].bitcast(BF16))
+
+        def turn_right(y, v, t, tags=("turn0", "turn1")):
+            if v == 0:
+                turn(("r", y, v, t), right0[:, t, :], right0[:, t + 4, :], tags)
+            else:
+                turn(("r", y, v, t), right1[:, 2 * t, :], right1[:, 2 * t + 1, :], tags)
+
+        def quantise_right(y, v, t):
+            quantise(("r", y, v, t), r_codes[y][v][:, t, :], r_scales[y][v][:, t, :])
+
+        def turn_left(pair, tags=("turn0", "turn1")):
+            y, n = divmod(2 * pair, NT)
+            turn(("l", pair), left[y][:, n, :], left[y][:, n + 1, :], tags)
+
+        def quantise_left(pair):
+            y, n = divmod(2 * pair, NT)
+            cols = slice(n * P, (n + 2) * P)
+            quantise(("l", pair), l_codes[y][:, cols], l_scales[y][:, cols])
+
+        def centres(pair, tags=("turn0", "turn1")):
+            bank = turn_bank(F32, tags)
+            for k in range(2):
+                x = 2 * pair + k
+                nc.tensor.transpose(bank[:, k * P : (k + 1) * P], centre[:, x : x + 1].to_broadcast([P, P]), ident32[:])
+            live[("ctr", pair)] = bank
+
+        def pooled_square(pair):
+            win = work.tile([P, 4, 256], F32, name="pooled_win", bufs=3)
+            for t in range(4):
+                nc.scalar.activation(
+                    out=win[:, t, :], in_=live[("ctr", pair)][:, 0:256], func=ACT.Square,
+                    scale=-1.0 / 256.0, bias=pos_bias[:, t : t + 1],
+                )
+            live[("pw", pair)] = win
+
+        def pooled_exp(pair):
+            win = live[("pw", pair)]
+            for t in range(4):
+                nc.scalar.activation(
+                    out=win[:, t, :], in_=win[:, t, :], func=ACT.Exp, scale=-0.5, bias=log_gain[:, 8 + t : 9 + t]
+                )
+
+        def exponent(x, g):
+            bank = psum.tile([P, 4, P], F32, name="expo%d" % g, tag="expo%d" % g)
+            for t in range(4):
+                nc.tensor.matmul(bank[:, t, :], lhsT=stationary[:, 4 * g + t, :], rhs=moving[:, x, :], start=True, stop=True)
+            live[("e", x, g)] = bank
+
+        def window(x, g):
+            win = work.tile([P, P, 4], F32, name="win", bufs=4)
+            nc.scalar.activation(
+                out=win[:], in_=live[("e", x, g)][:].rearrange("p t i -> p i t"), func=ACT.Exp, scale=1.0 / 16384.0
+            )
+            live[("w", x, g)] = win
+
+        def correlate(x, g):
+            y, n = divmod(x, NT)
+            cols = slice(n * P, (n + 1) * P)
+            bank = psum.tile([P, 4, P], F32, name="corr%d" % g, tag="corr%d" % g)
+            for t in range(4):
+                for e in (0, 1) if g == 2 else (g,):
+                    v = g // 2
+                    nc.tensor.matmul_mx(
+                        out=bank[:, t, :],
+                        lhsT=r_codes[y][v][:, t, e * P : (e + 1) * P].bitcast(FP8X4),
+                        lhsT_scale=r_scales[y][v][:, t, e * P : (e + 1) * P],
+                        rhs=l_codes[y][:, cols].bitcast(FP8X4),
+                        rhs_scale=l_scales[y][:, cols],
+                        start=(g < 2 or e == 0),
+                        stop=(g < 2 or e == 1),
+                    )
+            live[("c", x, g)] = bank
+
+        def begin(x):
+            live[("cg", x)] = work.tile([P, 3, 4 * P], BF16, name="cg", bufs=3, align_bytes=64)
+            live[("q", x)] = work.tile([P, 3, P], U32, name="cg_codes", bufs=3, align_bytes=64)
+            live[("s", x)] = work.tile([P, 3, P], U8, name="cg_scales", bufs=3, align_bytes=64)
+
+        def weigh(x, g):
+            if g == 2:
+                off = (x % 2) * P
+                win = live[("pw", x // 2)][:, :, off : off + P].rearrange("p t i -> p i t")
+            else:
+                win = live[("w", x, g)][:]
+            nc.vector.scalar_tensor_tensor(
+                live[("cg", x)][:, g, :].rearrange("p (i t) -> p i t", t=4),
+                live[("c", x, g)][:].rearrange("p t i -> p i t"),
+                (0.5 if g == 2 else 1.0) / math.sqrt(D),
+                win,
+                op0=ALU.mult,
+                op1=ALU.mult,
+            )
+
+        def quantise_cg(x, g0, g1):
+            nc.vector.quantize_mx(
+                out=live[("q", x)][:, g0:g1, :].rearrange("p g i -> p (g i)").bitcast(FP8X4),
+                scales=live[("s", x)][:, g0:g1, :].rearrange("p g i -> p (g i)"),
+                in_=live[("cg", x)][:, g0:g1, :].rearrange("p g i -> p (g i)"),
+            )
+
+        def project(x):
+            tag = "corr0" if x == TILES - 1 else "proj"
+            bank = psum.tile([P, F], F32, name=tag, tag=tag)
+            for k, g in enumerate((2, 0, 1)):
+                nc.tensor.matmul_mx(
+                    out=bank[:],
+                    lhsT=live[("q", x)][:, g, :].bitcast(FP8X4),
+                    lhsT_scale=live[("s", x)][:, g, :],
+                    rhs=w_words[:, g, :].bitcast(FP4X4),
+                    rhs_scale=w_scales[:, g, :],
+                    start=(k == 0),
+                    stop=(k == 2),
+                )
+            live[("o", x)] = bank
+
+        def offset(x):
+            term = work.tile([P, F], F32, name="term", bufs=3)
+            nc.vector.scalar_tensor_tensor(term[:], wd_row[:], disp_m1[:, x : x + 1], b_row[:], op0=ALU.mult, op1=ALU.add)
+            live[("t", x)] = term
+
+        def add(x, cols=slice(0, F)):
+            if cols.start == 0:
+                live[("p", x)] = work.tile([P, F], F32, name="pre", bufs=3)
+            pre = live[("p", x)]
+            if x not in BIAS_G:
+                nc.vector.tensor_tensor(pre[:, cols], live[("o", x)][:, cols], live[("t", x)][:, cols], op=ALU.add)
+                return
+            nc.vector.scalar_tensor_tensor(pre[:], wd_row[:], disp_m1[:, x : x + 1], live[("o", x)][:], op0=ALU.mult, op1=ALU.add)
+            full = work.tile([P, F], F32, name="full", bufs=3)
+            nc.gpsimd.tensor_tensor(full[:], pre[:], b_row[:], op=ALU.add)
+            live[("p", x)] = full
+
+        def finish(x, engine, cols=slice(0, F)):
+            y, n = divmod(x, NT)
+            if cols.start == 0:
+                live[("res", x)] = work.tile([P, F], F32, name="res", bufs=4)
+            res = live[("res", x)]
+            if engine == "V":
+                nc.vector.tensor_scalar(res[:, cols], live[("p", x)][:, cols], 0.0, None, op0=ALU.max)
+            elif engine == "G":
+                nc.gpsimd.tensor_scalar(res[:, cols], live[("p", x)][:, cols], 0.0, 0.0, op0=ALU.max, op1=ALU.add)
+            else:
+                nc.scalar.activation(out=res[:, cols], in_=live[("p", x)][:, cols], func=ACT.Relu)
+            nc.sync.dma_start(out=out[y].rearrange("(q n) f -> q n f", n=NT)[:, n, cols], in_=res[:, cols])
+
+        def turn_terms(h, tags):
+            bank = turn_bank(BF16, tags)
+            for k in range(8):
+                if h == 1:
+                    src = row_terms[:, k, :]
+                else:
+                    x = 4 * h + k
+                    src = col_terms[:, x * TERMS : x * TERMS + P]
+                nc.tensor.transpose(bank[:, k * P : (k + 1) * P], src, ident16[:])
+            live[("terms", h)] = bank
+
+        def empty_terms(h):
+            dst = stationary[:] if h == 1 else moving[:, 4 * h : 4 * h + 8, :]
+            nc.scalar.copy(out=dst.rearrange("p k i -> p (k i)"), in_=live[("terms", h)][:])
+
+
+        for t in range(4):
+            for s in (t, t + 4):
+                for block in range(4):
+                    widen(0, s, block, False)
+                    if small:
+                        small.pop(0)()
+            if t == 2:
+                turn_terms(1, ("expo1",))
+                turn_terms(0, ("expo0",))
+                empty_terms(1)
+                empty_terms(0)
+            turn_right(0, 0, t, (("turn0", "turn1", "corr1", "corr2")[t],))
+            empty(("r", 0, 0, t), True)
+            if t == 1:
+                turn_left(0, ("corr0",))
+                empty(("l", 0), False)
+        centres(0, ("proj",))
+        exponent(0, 0)
+        exponent(0, 1)
+        for k, t in enumerate((0, 2, 1, 3)):
+            flip(2 * t)
+            flip(2 * t + 1)
+            quantise_right(0, 0, k)
+            if k == 1:
+                quantise_left(0)
+        pooled_square(0)
+        window(0, 0)
+        window(0, 1)
+        for t, tag in ((0, "turn0"), (2, "turn1"), (1, "corr2"), (3, "proj")):
+            turn_right(0, 1, t, (tag,))
+            empty(("r", 0, 1, t), False, True)
+            if t == 1:
+                correlate(0, 0)
+                correlate(0, 1)
+        pooled_exp(0)
+        turns.clear()
+        turn_left(1)
+        centres(1)
+        exponent(1, 0)
+        exponent(1, 1)
+        empty(("l", 1), False)
+        for t in range(4):
+            quantise_right(0, 1, t)
+        pooled_square(1)
+        correlate(0, 2)
+        turn_left(2)
+        turn_terms(2, ("turn1",))
+        turns.clear()
+        quantise_left(1)
+        for s in (0, 4):
+            for block in range(4):
+                widen(1, s, block, False)
+        begin(0)
+
+        jobs = {
+            -1: [("l", 2)],
+            0: [("r", 1, 0, 0), ("r", 1, 0, 1)],
+            1: [("l", 3), ("c", 2)],
+            2: [("r", 1, 0, 2), ("r", 1, 0, 3)],
+            3: [("l", 4), ("c", 3)],
+            4: [("r", 1, 1, 0), ("r", 1, 1, 2)],
+            5: [("r", 1, 1, 1), ("r", 1, 1, 3)],
+            6: [("l", 5), ("c", 4)],
+            7: [("l", 6), ("c", 5)],
+            9: [("l", 7), ("c", 6)],
+            11: [("c", 7)],
+        }
+        exps = {0: 1, 3: 2, 5: 3, 7: 4, 9: 5, 11: 6, 13: 7}
+        flips = {1: (0, 1), 2: (4, 5), 3: (2, 3), 4: (6, 7)}
+
+        for x in range(TILES + 1):
+            if x >= 2:
+                add(x - 2)
+            if x >= 1:
+                project(x - 1)
+            for job in jobs.get(x - 1, []):
+                if job[0] != "c":
+                    empty(job, job[0] == "r" and job[2] == 0)
+            if x == 0:
+                empty_terms(2)
+            if x + 1 < TILES:
+                window(x + 1, 0)
+                window(x + 1, 1)
+            for job in jobs.get(x - 1, []):
+                if job[0] == "c":
+                    pooled_square(job[1])
+            if x in exps:
+                pooled_exp(exps[x])
+            for g in (0, 1, 2) if x % NT == 0 else (2, 0, 1):
+                if x < TILES:
+                    weigh(x, g)
+                if x + 1 < TILES:
+                    correlate(x + 1, g)
+            if x >= 3:
+                finish(x - 3, "V" if x - 3 in RELU_V else "S")
+            if x < 3:
+                for s in (x + 1, x + 5):
+                    for block in range(4):
+                        widen(1, s, block, block < WIDEN_S1)
+            for s in flips.get(x, ()):
+                flip(s)
+            for job in jobs.get(x - 1, []):
+                if job[0] == "l":
+                    quantise_left(job[1])
+                elif job[0] == "r":
+                    quantise_right(job[1], job[2], job[3])
+            for job in jobs.get(x, []):
+                if job[0] == "l":
+                    turn_left(job[1])
+                elif job[0] == "c":
+                    centres(job[1])
+                else:
+                    turn_right(job[1], job[2], job[3])
+            if x + 2 < TILES:
+                exponent(x + 2, 0)
+                exponent(x + 2, 1)
+            if x - 1 not in BIAS_G and 1 <= x:
+                offset(x - 1)
+            if x < TILES:
+                quantise_cg(x, 2, 3)
+                quantise_cg(x, 0, 2)
+            if x + 1 < TILES:
+                begin(x + 1)
+        last = TILES - 1
+        add(last, slice(0, F // 2))
+        add(last, slice(F // 2, F))
+        finish(last - 1, "S")
+        finish(last, "S", slice(0, F // 2))
+        finish(last, "V", slice(F // 2, F))

@@ -18,17 +18,19 @@ FP8X4 = mybir.dt.float8_e4m3fn_x4
 FP4X4 = mybir.dt.float4_e2m1fn_x4
 ALU = mybir.AluOpType
 ACT = mybir.ActivationFunctionType
+AXIS_X = mybir.AxisListType.X
 
 P = 128
-NT = 8
+NT = W // P
 TILES = H * NT
+LAST = TILES - 1
+POOLED = 2
 TERMS = 16
-BIAS_G = range(15)
-RELU_V = ()
-RELU_G = ()
-WIDEN_S0 = 0
-WIDEN_S1 = 0
-PERM = False
+ORIGIN = 512
+TWO_VAR = 128.0 * 128.0
+DISP_LIMIT = 1024.0
+LN_RANGE = 2.0**64
+TURN_BANKS = ("turn0", "turn1")
 
 
 def tile_stereocorrpyramidmotionencoder_d2p_kernel(
@@ -45,25 +47,25 @@ def tile_stereocorrpyramidmotionencoder_d2p_kernel(
             return keep.tile(shape, dtype, name=name, align_bytes=64)
 
         scale_all = kept("scale_all", [P, H * 8 * 4], F32)
-        gain_rows = kept("gain_rows", [P, 8], BF16)
+        gain_rows = kept("gain_rows", [P, NT], BF16)
         gain_k = kept("gain_k", [P, 3, 4], BF16)
         disp_i = kept("disp_i", [P, H, NT], BF16)
-        right_bytes = [kept("right_bytes%d" % y, [P, 8, D], U8) for y in range(H)]
+        right_bytes = [kept("right_bytes%d" % y, [P, NT, D], U8) for y in range(H)]
         left = [kept("left%d" % y, [P, NT, D], BF16) for y in range(H)]
         wd_row = kept("wd_row", [P, F], BF16)
         b_row = kept("b_row", [P, F], BF16)
         w_words = kept("w_words", [P, 3, 2 * F], U8)
         w_scales = kept("w_scales", [P, 3, F], U8)
 
-        nc.scalar.dma_start(out=scale_all[:], in_=f_right_scale.rearrange("y j d -> (y j d)").partition_broadcast(P))
-        nc.scalar.dma_start(out=gain_rows[:], in_=gain[0:W].rearrange("(m s) -> m s", s=8))
+        nc.sync.dma_start(out=scale_all[:], in_=f_right_scale.rearrange("y j d -> (y j d)").partition_broadcast(P))
+        nc.sync.dma_start(out=gain_rows[:], in_=gain[0:W].rearrange("(m s) -> m s", s=NT))
         nc.scalar.dma_start(out=gain_k[:], in_=gain.rearrange("(g p t) -> p g t", p=P, t=4))
         nc.scalar.dma_start(out=disp_i[:], in_=disp.rearrange("y (q n) -> q y n", n=NT))
 
-        def load_right(y, h):
+        def load_right(y, half):
             src = f_right_bytes[y].rearrange("(m a b c) d -> m a b (c d)", a=2, b=2, c=2)
             dst = right_bytes[y][:].rearrange("m (a b c) d -> m a b (c d)", a=2, b=2)
-            nc.sync.dma_start(out=dst[:, :, h, :], in_=src[:, :, h, :])
+            nc.sync.dma_start(out=dst[:, :, half, :], in_=src[:, :, half, :])
 
         def load_left(y, n0, n1):
             src = f_left[y].rearrange("(q n) d -> q n d", n=NT)
@@ -72,14 +74,13 @@ def tile_stereocorrpyramidmotionencoder_d2p_kernel(
         nc.vector.memset(w_scales[:].rearrange("p g n -> p (g n)").bitcast(I32), 0)
         load_right(0, 0)
         load_right(0, 1)
-        load_left(0, 0, 2)
-        load_left(0, 2, 4)
-        load_left(0, 4, 6)
+        for n0 in (0, 2, 4):
+            load_left(0, n0, n0 + 2)
         load_right(1, 0)
-        for quad in range(4):
+        for quadrant in range(4):
             nc.sync.dma_start(
-                out=w_scales[32 * quad : 32 * quad + 4, :, :].bitcast(I32),
-                in_=w_corr_scales[:, 4 * quad : 4 * quad + 4, :].rearrange("g r n -> r g n").bitcast(I32),
+                out=w_scales[32 * quadrant : 32 * quadrant + 4, :, :].bitcast(I32),
+                in_=w_corr_scales[:, 4 * quadrant : 4 * quadrant + 4, :].rearrange("g r n -> r g n").bitcast(I32),
             )
         nc.sync.dma_start(out=w_words[:].bitcast(I32), in_=w_corr_words.rearrange("g p n -> p g n").bitcast(I32))
         nc.sync.dma_start(out=wd_row[:], in_=w_disp.partition_broadcast(P))
@@ -89,281 +90,282 @@ def tile_stereocorrpyramidmotionencoder_d2p_kernel(
         load_left(1, 0, 4)
         load_left(1, 4, 8)
 
-        def counted(name, pattern, base, step):
-            t = kept(name, [P] + [n for (s, n) in pattern], F32)
-            nc.gpsimd.iota(t[:], pattern, base=base, channel_multiplier=step, allow_small_or_imprecise_dtypes=True)
-            return t
+        def counted(name, pattern, step):
+            tile = kept(name, [P] + [count for (stride, count) in pattern], F32)
+            nc.gpsimd.iota(tile[:], pattern, base=-ORIGIN, channel_multiplier=step, allow_small_or_imprecise_dtypes=True)
+            return tile[:].rearrange("p a b -> p (a b)")
 
         ident32 = kept("ident32", [P, P], F32)
         make_identity(nc, ident32[:])
-        c_int = counted("c_int", [[0, H], [1, NT]], -512, 8)
-        j_int = counted("j_int", [[512, 2], [1, 4]], -512, 4)
+        pixel = counted("pixel", [[0, H], [1, NT]], 8)
+        tap = counted("tap", [[512, 2], [1, 4]], 4)
         ident16 = kept("ident16", [P, P], BF16)
-        c_flat = c_int[:].rearrange("p y n -> p (y n)")
-        j_flat = j_int[:].rearrange("p g t -> p (g t)")
-        c_high = c_flat[:, 0:1]
+        pixel_high = pixel[:, 0:1]
 
-        col_terms = kept("col_terms", [P, TILES * TERMS + P - TERMS], BF16)
-        row_terms = kept("row_terms", [P, 8, P], BF16)
-        col_v = col_terms[:, 0 : TILES * TERMS].rearrange("p (x k) -> p x k", k=TERMS)
-        row_v = row_terms[:].rearrange("p (g t) k -> p g t k", t=4)
+        pixel_terms = kept("pixel_terms", [P, TILES * TERMS + P - TERMS], BF16)
+        tap_terms = kept("tap_terms", [P, 8, P], BF16)
+        pixel_v = pixel_terms[:, 0 : TILES * TERMS].rearrange("p (x k) -> p x k", k=TERMS)
+        tap_v = tap_terms[:].rearrange("p (g t) k -> p g t k", t=4)
         pick = kept("pick", [P, 8], F32)
-        half_j2 = kept("half_j2", [P, 8], F32)
-        pos_bias = kept("pos_bias", [P, 4], F32)
-        nc.vector.memset(col_terms[:], 0.0)
-        nc.vector.memset(row_terms[:], 0.0)
-        nc.vector.tensor_reduce(pick[:], ident32[:].rearrange("p (j r) -> p j r", r=16), axis=mybir.AxisListType.X, op=ALU.add)
-        nc.vector.memset(row_terms[:, :, 6:9], 1.0)
+        half_tap2 = kept("half_tap2", [P, 8], F32)
+        pooled_pos = kept("pooled_pos", [P, 4], F32)
+        nc.vector.memset(pixel_terms[:], 0.0)
+        nc.vector.memset(tap_terms[:], 0.0)
+        nc.vector.tensor_reduce(pick[:], ident32[:].rearrange("p (b r) -> p b r", r=16), axis=AXIS_X, op=ALU.add)
+        nc.vector.memset(tap_terms[:, :, 6:9], 1.0)
+        nc.vector.memset(pixel_v[:, :, 9:12], 1.0)
         nc.vector.tensor_copy(out=ident16[:], in_=ident32[:])
-        nc.vector.tensor_copy(out=col_v[:, :, 0:6:3], in_=c_high.unsqueeze(2).to_broadcast([P, TILES, 2]))
-        nc.vector.tensor_scalar(col_v[:, :, 1:6:3], c_flat.unsqueeze(2).to_broadcast([P, TILES, 2]), c_high, None, op0=ALU.subtract)
+        nc.vector.tensor_copy(out=pixel_v[:, :, 0:6:3], in_=pixel_high.unsqueeze(2).to_broadcast([P, TILES, 2]))
+        nc.vector.tensor_scalar(
+            pixel_v[:, :, 1:6:3], pixel.unsqueeze(2).to_broadcast([P, TILES, 2]), pixel_high, None, op0=ALU.subtract
+        )
         for g in range(2):
-            nc.vector.tensor_copy(out=row_v[:, g, :, 0:3], in_=j_int[:, g, 0:1].unsqueeze(2).to_broadcast([P, 4, 3]))
-            nc.vector.tensor_scalar(
-                row_v[:, g, :, 3:6], c_flat[:, 0:4].unsqueeze(2).to_broadcast([P, 4, 3]), c_high, None, op0=ALU.subtract
+            nc.vector.tensor_copy(
+                out=tap_v[:, g, :, 0:3], in_=tap[:, 4 * g : 4 * g + 1].unsqueeze(2).to_broadcast([P, 4, 3])
             )
-        nc.vector.scalar_tensor_tensor(half_j2[:], j_flat, -0.5, j_flat, op0=ALU.mult, op1=ALU.mult)
-        nc.vector.tensor_scalar(pos_bias[:], j_int[:, 1, :], 1.0 / 128.0, (0.5 - 512.0) / 256.0, op0=ALU.mult, op1=ALU.add)
+            nc.vector.tensor_scalar(
+                tap_v[:, g, :, 3:6], pixel[:, 0:4].unsqueeze(2).to_broadcast([P, 4, 3]), pixel_high, None, op0=ALU.subtract
+            )
+        nc.vector.scalar_tensor_tensor(half_tap2[:], tap, -0.5, tap, op0=ALU.mult, op1=ALU.mult)
+        nc.vector.tensor_scalar(pooled_pos[:], tap[:, 4:8], 1.0 / 128.0, (0.5 - ORIGIN) / 256.0, op0=ALU.mult, op1=ALU.add)
 
         picked = kept("picked", [P, H, 4, 8], F32)
         scale_m = kept("scale_m", [P, H * 4], F32)
-        sign_rows = kept("sign_rows", [P, 8], F32)
-        sign_pool = kept("sign_pool", [P, 4], F32)
-        scale_signed = kept("scale_signed", [P, H, 8, 4], F32)
+        half_sign = kept("half_sign", [P, NT], F32)
+        half_sign_pooled = kept("half_sign_pooled", [P, 4], F32)
+        scale_signed = kept("scale_signed", [P, H, NT, 4], F32)
         resign = kept("resign", [P, 4, 2], F32)
         gain_abs = kept("gain_abs", [P, 12], F32)
         factors = kept("factors", [P, 3, 12], F32)
         logs = kept("logs", [P, 3, 12], F32)
         log_gain = kept("log_gain", [P, 12], F32)
-        log_part = kept("log_part", [P, 12], F32)
-        disp_c = kept("disp_c", [P, TILES], F32)
+        low_part = kept("low_part", [P, 12], F32)
+        disp_clamped = kept("disp_clamped", [P, TILES], F32)
         disp_m1 = kept("disp_m1", [P, TILES], F32)
         centre = kept("centre", [P, TILES], F32)
         whole = kept("whole", [P, TILES + 8], F32)
         rest1 = kept("rest1", [P, TILES + 8], F32)
         rest2 = kept("rest2", [P, TILES + 8], F32)
         pieces = kept("pieces", [P, 3, TILES + 8], BF16)
+        one = kept("one", [P, 1], F32)
         gain_flat = gain_k[:].rearrange("p g t -> p (g t)")
         disp_flat = disp_i[:].rearrange("p y n -> p (y n)")
 
-        small = [
-            lambda: nc.vector.tensor_tensor(
-                picked[:],
-                scale_all[:].rearrange("p (y j d) -> p y d j", y=H, d=4),
-                pick[:].unsqueeze(1).unsqueeze(1).to_broadcast([P, H, 4, 8]),
-                op=ALU.mult,
-            ),
-            lambda: nc.vector.tensor_scalar(sign_rows[:], gain_rows[:], 0.0, 0.5, op0=ALU.is_ge, op1=ALU.subtract),
-            lambda: nc.vector.tensor_reduce(
-                scale_m[:], picked[:].rearrange("p y d j -> p (y d) j"), axis=mybir.AxisListType.X, op=ALU.add
-            ),
-            lambda: nc.vector.scalar_tensor_tensor(gain_abs[:], gain_flat, -1.0, gain_flat, op0=ALU.mult, op1=ALU.max),
-            lambda: nc.vector.scalar_tensor_tensor(
-                scale_signed[:, 0, :, :],
-                scale_m[:, 0:4].unsqueeze(1).to_broadcast([P, 8, 4]),
+        def sign_scales(y):
+            nc.vector.scalar_tensor_tensor(
+                scale_signed[:, y, :, :],
+                scale_m[:, 4 * y : 4 * y + 4].unsqueeze(1).to_broadcast([P, NT, 4]),
                 2.0,
-                sign_rows[:].unsqueeze(2).to_broadcast([P, 8, 4]),
+                half_sign[:].unsqueeze(2).to_broadcast([P, NT, 4]),
                 op0=ALU.mult,
                 op1=ALU.mult,
-            ),
-            lambda: nc.vector.tensor_scalar(factors[:, 0, :], gain_abs[:], 2.0**-64, 2.0**64, op0=ALU.max, op1=ALU.min),
-            lambda: nc.vector.tensor_scalar(factors[:, 1, :], gain_abs[:], 2.0**-64, 1.0, op0=ALU.mult, op1=ALU.max),
-            lambda: nc.vector.tensor_scalar(log_part[:], gain_abs[:], 2.0**-64, 2.0**64, op0=ALU.min, op1=ALU.mult),
-            lambda: nc.vector.tensor_scalar(sign_pool[:], gain_k[:, 2, :], 0.0, 0.5, op0=ALU.is_ge, op1=ALU.subtract),
-            lambda: nc.vector.tensor_scalar(factors[:, 2, :], log_part[:], 2.0**-64, None, op0=ALU.max),
-        ]
-        for step in small:
-            step()
+            )
+
+        nc.vector.tensor_tensor(
+            picked[:],
+            scale_all[:].rearrange("p (y b d) -> p y d b", y=H, d=4),
+            pick[:].unsqueeze(1).unsqueeze(1).to_broadcast([P, H, 4, 8]),
+            op=ALU.mult,
+        )
+        nc.vector.tensor_scalar(half_sign[:], gain_rows[:], 0.0, 0.5, op0=ALU.is_ge, op1=ALU.subtract)
+        nc.vector.scalar_tensor_tensor(gain_abs[:], gain_flat, -1.0, gain_flat, op0=ALU.mult, op1=ALU.max)
+        nc.vector.tensor_reduce(scale_m[:], picked[:].rearrange("p y d b -> p (y d) b"), axis=AXIS_X, op=ALU.add)
+        nc.vector.tensor_scalar(low_part[:], gain_abs[:], 1.0 / LN_RANGE, LN_RANGE, op0=ALU.min, op1=ALU.mult)
+        nc.vector.tensor_scalar(factors[:, 0, :], gain_abs[:], 1.0 / LN_RANGE, LN_RANGE, op0=ALU.max, op1=ALU.min)
+        sign_scales(0)
+        nc.vector.tensor_scalar(factors[:, 1, :], gain_abs[:], 1.0 / LN_RANGE, 1.0, op0=ALU.mult, op1=ALU.max)
+        nc.vector.tensor_scalar(factors[:, 2, :], low_part[:], 1.0 / LN_RANGE, None, op0=ALU.max)
         nc.scalar.activation(out=logs[:], in_=factors[:], func=ACT.Ln)
-        one = kept("one", [P, 1], F32)
         nc.scalar.activation(out=one[:], in_=logs[:, 0, 0:1], func=ACT.Exp, scale=0.0)
 
-        small = [
+        between = [
+            lambda: nc.vector.tensor_scalar(disp_clamped[:], disp_flat, DISP_LIMIT, -DISP_LIMIT, op0=ALU.min, op1=ALU.max),
+            lambda: nc.vector.tensor_scalar(half_sign_pooled[:], gain_k[:, POOLED, :], 0.0, 0.5, op0=ALU.is_ge, op1=ALU.subtract),
+            lambda: nc.vector.scalar_tensor_tensor(centre[:], disp_clamped[:], -128.0, pixel, op0=ALU.mult, op1=ALU.add),
             lambda: nc.vector.scalar_tensor_tensor(
                 resign[:],
-                sign_rows[:].rearrange("p (t e) -> p t e", e=2),
+                half_sign[:].rearrange("p (t e) -> p t e", e=2),
                 4.0,
-                sign_pool[:].unsqueeze(2).to_broadcast([P, 4, 2]),
+                half_sign_pooled[:].unsqueeze(2).to_broadcast([P, 4, 2]),
                 op0=ALU.mult,
                 op1=ALU.mult,
             ),
-            lambda: nc.vector.tensor_scalar(disp_c[:], disp_flat, 1024.0, -1024.0, op0=ALU.min, op1=ALU.max),
-            lambda: nc.vector.tensor_reduce(
-                log_gain[:], logs[:].rearrange("p r k -> p k r"), axis=mybir.AxisListType.X, op=ALU.add
-            ),
-            lambda: nc.vector.scalar_tensor_tensor(
-                centre[:], disp_c[:], -128.0, c_flat, op0=ALU.mult, op1=ALU.add
-            ),
-            lambda: nc.vector.scalar_tensor_tensor(
-                whole[:, TILES:], log_gain[:, 0:8], 16384.0, half_j2[:], op0=ALU.mult, op1=ALU.add
+            lambda: nc.vector.tensor_scalar(
+                pixel_v[:, :, 2:6:3], disp_clamped[:].unsqueeze(2).to_broadcast([P, TILES, 2]), -128.0, None, op0=ALU.mult
             ),
             lambda: nc.vector.scalar_tensor_tensor(whole[:, 0:TILES], centre[:], -0.5, centre[:], op0=ALU.mult, op1=ALU.mult),
-            lambda: nc.vector.tensor_scalar(
-                col_v[:, :, 2:6:3], disp_c[:].unsqueeze(2).to_broadcast([P, TILES, 2]), -128.0, None, op0=ALU.mult
-            ),
-            lambda: nc.vector.tensor_copy(out=pieces[:, 0, :], in_=whole[:]),
-            lambda: nc.vector.tensor_tensor(rest1[:], whole[:], pieces[:, 0, :], op=ALU.subtract),
-            lambda: nc.vector.tensor_copy(out=pieces[:, 1, :], in_=rest1[:]),
-            lambda: nc.vector.tensor_tensor(rest2[:], rest1[:], pieces[:, 1, :], op=ALU.subtract),
-            lambda: nc.vector.tensor_copy(out=pieces[:, 2, :], in_=rest2[:]),
-            lambda: nc.vector.tensor_copy(out=col_v[:, :, 6:9], in_=pieces[:, :, 0:TILES].rearrange("p r x -> p x r")),
-            lambda: nc.vector.tensor_copy(out=row_terms[:, :, 9:12], in_=pieces[:, :, TILES:].rearrange("p r x -> p x r")),
-            lambda: nc.vector.tensor_copy(out=col_v[:, :, 9:12], in_=one[:].unsqueeze(2).to_broadcast([P, TILES, 3])),
-            lambda: nc.vector.tensor_scalar(disp_m1[:], disp_flat, 1.0, None, op0=ALU.subtract),
+            lambda: nc.vector.tensor_reduce(log_gain[:], logs[:].rearrange("p r k -> p k r"), axis=AXIS_X, op=ALU.add),
+            None,
             lambda: nc.vector.scalar_tensor_tensor(
-                scale_signed[:, 1, :, :],
-                scale_m[:, 4:8].unsqueeze(1).to_broadcast([P, 8, 4]),
-                2.0,
-                sign_rows[:].unsqueeze(2).to_broadcast([P, 8, 4]),
-                op0=ALU.mult,
-                op1=ALU.mult,
+                whole[:, TILES:], log_gain[:, 0:8], TWO_VAR, half_tap2[:], op0=ALU.mult, op1=ALU.add
             ),
+            lambda: sign_scales(1),
+            lambda: nc.vector.tensor_copy(out=pieces[:, 0, :], in_=whole[:]),
+            None,
+            lambda: nc.vector.tensor_tensor(rest1[:], whole[:], pieces[:, 0, :], op=ALU.subtract),
+            None,
+            lambda: nc.vector.tensor_copy(out=pieces[:, 1, :], in_=rest1[:]),
+            None,
+            lambda: nc.vector.tensor_tensor(rest2[:], rest1[:], pieces[:, 1, :], op=ALU.subtract),
+            None,
+            lambda: nc.vector.tensor_copy(out=pieces[:, 2, :], in_=rest2[:]),
+            None,
+            lambda: nc.vector.tensor_copy(out=tap_terms[:, :, 9:12], in_=pieces[:, :, TILES:].rearrange("p r x -> p x r")),
+            lambda: nc.vector.tensor_copy(out=pixel_v[:, :, 6:9], in_=pieces[:, :, 0:TILES].rearrange("p r x -> p x r")),
+            lambda: nc.vector.tensor_scalar(disp_m1[:], disp_flat, one[:], None, op0=ALU.subtract),
         ]
 
-        right0 = kept("right0", [P, 8, D], BF16)
-        right1 = kept("right1", [P, 8, D], BF16)
-        r_codes = [[kept("r_codes%d%d" % (y, v), [P, 4, 256], U32) for v in range(2)] for y in range(H)]
-        r_scales = [[kept("r_scales%d%d" % (y, v), [P, 4, 256], U8) for v in range(2)] for y in range(H)]
+        right_rows = [kept("right_rows%d" % level, [P, NT, D], BF16) for level in range(2)]
+        r_codes = [[kept("r_codes%d%d" % (y, level), [P, 4, 256], U32) for level in range(2)] for y in range(H)]
+        r_scales = [[kept("r_scales%d%d" % (y, level), [P, 4, 256], U8) for level in range(2)] for y in range(H)]
         l_codes = [kept("l_codes%d" % y, [P, W], U32) for y in range(H)]
         l_scales = [kept("l_scales%d" % y, [P, W], U8) for y in range(H)]
         moving = kept("moving", [P, TILES, P], BF16)
         stationary = kept("stationary", [P, 8, P], BF16)
         live = {}
-        turns = []
 
-        def widen(y, s, block, on_scalar):
-            cols = slice(block * P, (block + 1) * P)
-            src = right_bytes[y][:, s, cols].bitcast(FP8)
-            factor = scale_signed[:, y, s, block : block + 1]
-            if on_scalar:
-                nc.scalar.activation(out=right0[:, s, cols], in_=src, func=ACT.Copy, scale=factor)
-            elif PERM:
-                dst = right0[:, s, :].rearrange("p (u w e) -> p w u e", u=2, e=2)[:, block * 32 : (block + 1) * 32, :, :]
-                nc.vector.tensor_scalar(dst, src.rearrange("p (w u e) -> p w u e", u=2, e=2), factor, None, op0=ALU.mult)
-            else:
-                nc.vector.tensor_scalar(right0[:, s, cols], src, factor, None, op0=ALU.mult)
+        def bank_tile(shape, dtype, bank):
+            return psum.tile(shape, dtype, name=bank, tag=bank)
+
+        def widen(y, s):
+            rows = right_rows[0][:, s, :].rearrange("p (u w e) -> p w u e", u=2, e=2)
+            for block in range(4):
+                src = right_bytes[y][:, s, block * P : (block + 1) * P].bitcast(FP8)
+                nc.vector.tensor_scalar(
+                    rows[:, block * 32 : (block + 1) * 32, :, :],
+                    src.rearrange("p (w u e) -> p w u e", u=2, e=2),
+                    scale_signed[:, y, s, block : block + 1],
+                    None,
+                    op0=ALU.mult,
+                )
+                step = between.pop(0) if between else None
+                if step:
+                    step()
 
         def flip(s):
-            nc.vector.tensor_scalar(right1[:, s, :], right0[:, s, :], resign[:, s // 2, s % 2 : s % 2 + 1], None, op0=ALU.mult)
+            nc.vector.tensor_scalar(
+                right_rows[1][:, s, :], right_rows[0][:, s, :], resign[:, s // 2, s % 2 : s % 2 + 1], None, op0=ALU.mult
+            )
 
-        def turn_bank(dtype, tags):
-            tag = tags[len(turns) % len(tags)]
-            turns.append(tag)
-            return psum.tile([P, 512 if dtype == F32 else 1024], dtype, name=tag, tag=tag)
-
-        def turn(key, rows_a, rows_b, tags=("turn0", "turn1")):
-            bank = turn_bank(F32, tags)
-            for a, rows in enumerate((rows_a, rows_b)):
-                words = rows.bitcast(F32)
-                for u in range(2):
-                    src = words[:, u * P : (u + 1) * P] if (PERM and key[0] == "r") else words[:, u : 256 : 2]
-                    nc.tensor.transpose(bank[:, (2 * a + u) * P : (2 * a + u + 1) * P], src, ident32[:])
-            live[key] = bank
-
-        def empty(key, weave, on_vector=False):
-            grouped = work.tile([P, 512], F32, name="grouped", bufs=6, align_bytes=64)
-            if weave:
-                src = live[key][:].rearrange("p (a r) -> p r a", a=4)
-                dst = grouped[:].rearrange("p (r a) -> p r a", a=4)
+        def turn(job, bank):
+            if job[0] in ("pixel", "tap"):
+                tile = bank_tile([P, 8 * P], BF16, bank)
+                if job[0] == "tap":
+                    sources = [tap_terms[:, k, :] for k in range(8)]
+                else:
+                    sources = [pixel_terms[:, x * TERMS : x * TERMS + P] for x in range(job[1], job[2])]
+                identity = ident16
             else:
-                src = live[key][:].rearrange("p (e u r) -> p e r u", e=2, u=2)
-                dst = grouped[:].rearrange("p (e r u) -> p e r u", e=2, u=2)
-            if on_vector:
-                nc.vector.tensor_copy(out=dst, in_=src)
-            else:
-                nc.scalar.copy(out=dst, in_=src)
-            live[key] = grouped
+                tile = bank_tile([P, 4 * P], F32, bank)
+                identity = ident32
+                if job[0] == "centre":
+                    sources = [centre[:, x : x + 1].to_broadcast([P, P]) for x in (2 * job[1], 2 * job[1] + 1)]
+                elif job[0] == "left":
+                    y, n = divmod(2 * job[1], NT)
+                    sources = [left[y][:, n + a, :].bitcast(F32)[:, u:256:2] for a in range(2) for u in range(2)]
+                else:
+                    level, t = job[2:]
+                    rows = (2 * t, 2 * t + 1) if level else (t, t + 4)
+                    sources = [right_rows[level][:, s, :].bitcast(F32)[:, u * P : (u + 1) * P] for s in rows for u in range(2)]
+            for k, source in enumerate(sources):
+                nc.tensor.transpose(tile[:, k * P : (k + 1) * P], source, identity[:])
+            live[job] = tile
 
-        def quantise(key, codes, scales):
-            nc.vector.quantize_mx(out=codes.bitcast(FP8X4), scales=scales, in_=live[key][:].bitcast(BF16))
-
-        def turn_right(y, v, t, tags=("turn0", "turn1")):
-            if v == 0:
-                turn(("r", y, v, t), right0[:, t, :], right0[:, t + 4, :], tags)
-            else:
-                turn(("r", y, v, t), right1[:, 2 * t, :], right1[:, 2 * t + 1, :], tags)
-
-        def quantise_right(y, v, t):
-            quantise(("r", y, v, t), r_codes[y][v][:, t, :], r_scales[y][v][:, t, :])
-
-        def turn_left(pair, tags=("turn0", "turn1")):
-            y, n = divmod(2 * pair, NT)
-            turn(("l", pair), left[y][:, n, :], left[y][:, n + 1, :], tags)
-
-        def quantise_left(pair):
-            y, n = divmod(2 * pair, NT)
-            cols = slice(n * P, (n + 2) * P)
-            quantise(("l", pair), l_codes[y][:, cols], l_scales[y][:, cols])
-
-        def centres(pair, tags=("turn0", "turn1")):
-            bank = turn_bank(F32, tags)
-            for k in range(2):
-                x = 2 * pair + k
-                nc.tensor.transpose(bank[:, k * P : (k + 1) * P], centre[:, x : x + 1].to_broadcast([P, P]), ident32[:])
-            live[("ctr", pair)] = bank
-
-        def pooled_square(pair):
-            win = work.tile([P, 4, 256], F32, name="pooled_win", bufs=3)
-            for t in range(4):
-                nc.scalar.activation(
-                    out=win[:, t, :], in_=live[("ctr", pair)][:, 0:256], func=ACT.Square,
-                    scale=-1.0 / 256.0, bias=pos_bias[:, t : t + 1],
+        def empty(job):
+            tile = live[job]
+            if job[0] == "tap":
+                nc.scalar.copy(out=stationary[:].rearrange("p k i -> p (k i)"), in_=tile[:])
+            elif job[0] == "pixel":
+                nc.scalar.copy(
+                    out=moving[:, job[1] : job[2], :].rearrange("p k i -> p (k i)"), in_=tile[:, 0 : (job[2] - job[1]) * P]
                 )
-            live[("pw", pair)] = win
+            elif job[0] == "centre":
+                squares = work.tile([P, 4, 2 * P], F32, name="pooled_win", bufs=3)
+                for t in range(4):
+                    nc.scalar.activation(
+                        out=squares[:, t, :],
+                        in_=tile[:, 0 : 2 * P],
+                        func=ACT.Square,
+                        scale=-1.0 / 256.0,
+                        bias=pooled_pos[:, t : t + 1],
+                    )
+                live[("pooled_win", job[1])] = squares
+            else:
+                grouped = work.tile([P, 4 * P], F32, name="grouped", bufs=8, align_bytes=64)
+                if job[0] == "right" and job[2] == 0:
+                    nc.scalar.copy(
+                        out=grouped[:].rearrange("p (m a) -> p m a", a=4), in_=tile[:].rearrange("p (a m) -> p m a", a=4)
+                    )
+                else:
+                    nc.scalar.copy(
+                        out=grouped[:].rearrange("p (e m u) -> p e m u", e=2, u=2),
+                        in_=tile[:].rearrange("p (e u m) -> p e m u", e=2, u=2),
+                    )
+                live[job] = grouped
 
-        def pooled_exp(pair):
-            win = live[("pw", pair)]
+        def quantise(job):
+            if job[0] == "left":
+                y, n = divmod(2 * job[1], NT)
+                codes, scales = l_codes[y][:, n * P : (n + 2) * P], l_scales[y][:, n * P : (n + 2) * P]
+            else:
+                y, level, t = job[1:]
+                codes, scales = r_codes[y][level][:, t, :], r_scales[y][level][:, t, :]
+            nc.vector.quantize_mx(out=codes.bitcast(FP8X4), scales=scales, in_=live[job][:].bitcast(BF16))
+
+        def pooled_window(pair):
+            win = live[("pooled_win", pair)]
             for t in range(4):
                 nc.scalar.activation(
                     out=win[:, t, :], in_=win[:, t, :], func=ACT.Exp, scale=-0.5, bias=log_gain[:, 8 + t : 9 + t]
                 )
 
         def exponent(x, g):
-            bank = psum.tile([P, 4, P], F32, name="expo%d" % g, tag="expo%d" % g)
+            tile = bank_tile([P, 4, P], F32, "expo%d" % g)
             for t in range(4):
-                nc.tensor.matmul(bank[:, t, :], lhsT=stationary[:, 4 * g + t, :], rhs=moving[:, x, :], start=True, stop=True)
-            live[("e", x, g)] = bank
+                nc.tensor.matmul(tile[:, t, :], lhsT=stationary[:, 4 * g + t, :], rhs=moving[:, x, :], start=True, stop=True)
+            live[("expo", x, g)] = tile
 
         def window(x, g):
-            win = work.tile([P, P, 4], F32, name="win", bufs=4)
+            win = work.tile([P, P, 4], F32, name="win", bufs=8)
             nc.scalar.activation(
-                out=win[:], in_=live[("e", x, g)][:].rearrange("p t i -> p i t"), func=ACT.Exp, scale=1.0 / 16384.0
+                out=win[:], in_=live[("expo", x, g)][:].rearrange("p t q -> p q t"), func=ACT.Exp, scale=1.0 / TWO_VAR
             )
-            live[("w", x, g)] = win
+            live[("win", x, g)] = win
 
         def correlate(x, g):
             y, n = divmod(x, NT)
             cols = slice(n * P, (n + 1) * P)
-            bank = psum.tile([P, 4, P], F32, name="corr%d" % g, tag="corr%d" % g)
+            level = g // POOLED
+            halves = (0, 1) if level else (g,)
+            tile = bank_tile([P, 4, P], F32, "corr%d" % g)
             for t in range(4):
-                for e in (0, 1) if g == 2 else (g,):
-                    v = g // 2
+                for e in halves:
                     nc.tensor.matmul_mx(
-                        out=bank[:, t, :],
-                        lhsT=r_codes[y][v][:, t, e * P : (e + 1) * P].bitcast(FP8X4),
-                        lhsT_scale=r_scales[y][v][:, t, e * P : (e + 1) * P],
+                        out=tile[:, t, :],
+                        lhsT=r_codes[y][level][:, t, e * P : (e + 1) * P].bitcast(FP8X4),
+                        lhsT_scale=r_scales[y][level][:, t, e * P : (e + 1) * P],
                         rhs=l_codes[y][:, cols].bitcast(FP8X4),
                         rhs_scale=l_scales[y][:, cols],
-                        start=(g < 2 or e == 0),
-                        stop=(g < 2 or e == 1),
+                        start=(e == halves[0]),
+                        stop=(e == halves[-1]),
                     )
-            live[("c", x, g)] = bank
+            live[("corr", x, g)] = tile
 
         def begin(x):
-            live[("cg", x)] = work.tile([P, 3, 4 * P], BF16, name="cg", bufs=3, align_bytes=64)
-            live[("q", x)] = work.tile([P, 3, P], U32, name="cg_codes", bufs=3, align_bytes=64)
-            live[("s", x)] = work.tile([P, 3, P], U8, name="cg_scales", bufs=3, align_bytes=64)
+            live[("cg", x)] = work.tile([P, 3, 4 * P], BF16, name="cg", bufs=4, align_bytes=64)
+            live[("cg_codes", x)] = work.tile([P, 3, P], U32, name="cg_codes", bufs=4, align_bytes=64)
+            live[("cg_scales", x)] = work.tile([P, 3, P], U8, name="cg_scales", bufs=4, align_bytes=64)
 
         def weigh(x, g):
-            if g == 2:
-                off = (x % 2) * P
-                win = live[("pw", x // 2)][:, :, off : off + P].rearrange("p t i -> p i t")
+            if g == POOLED:
+                first = (x % 2) * P
+                win = live[("pooled_win", x // 2)][:, :, first : first + P].rearrange("p t q -> p q t")
             else:
-                win = live[("w", x, g)][:]
+                win = live[("win", x, g)][:]
             nc.vector.scalar_tensor_tensor(
-                live[("cg", x)][:, g, :].rearrange("p (i t) -> p i t", t=4),
-                live[("c", x, g)][:].rearrange("p t i -> p i t"),
-                (0.5 if g == 2 else 1.0) / math.sqrt(D),
+                live[("cg", x)][:, g, :].rearrange("p (q t) -> p q t", t=4),
+                live[("corr", x, g)][:].rearrange("p t q -> p q t"),
+                (0.5 if g == POOLED else 1.0) / math.sqrt(D),
                 win,
                 op0=ALU.mult,
                 op1=ALU.mult,
@@ -371,198 +373,201 @@ def tile_stereocorrpyramidmotionencoder_d2p_kernel(
 
         def quantise_cg(x, g0, g1):
             nc.vector.quantize_mx(
-                out=live[("q", x)][:, g0:g1, :].rearrange("p g i -> p (g i)").bitcast(FP8X4),
-                scales=live[("s", x)][:, g0:g1, :].rearrange("p g i -> p (g i)"),
-                in_=live[("cg", x)][:, g0:g1, :].rearrange("p g i -> p (g i)"),
+                out=live[("cg_codes", x)][:, g0:g1, :].rearrange("p g q -> p (g q)").bitcast(FP8X4),
+                scales=live[("cg_scales", x)][:, g0:g1, :].rearrange("p g q -> p (g q)"),
+                in_=live[("cg", x)][:, g0:g1, :].rearrange("p g c -> p (g c)"),
             )
 
-        def project(x):
-            tag = "corr0" if x == TILES - 1 else "proj"
-            bank = psum.tile([P, F], F32, name=tag, tag=tag)
-            for k, g in enumerate((2, 0, 1)):
+        def project(x, passes=(POOLED, 0, 1)):
+            if passes[0] == POOLED:
+                live[("proj", x)] = bank_tile([P, F], F32, "expo0" if x == LAST else "proj")
+            for g in passes:
                 nc.tensor.matmul_mx(
-                    out=bank[:],
-                    lhsT=live[("q", x)][:, g, :].bitcast(FP8X4),
-                    lhsT_scale=live[("s", x)][:, g, :],
+                    out=live[("proj", x)][:],
+                    lhsT=live[("cg_codes", x)][:, g, :].bitcast(FP8X4),
+                    lhsT_scale=live[("cg_scales", x)][:, g, :],
                     rhs=w_words[:, g, :].bitcast(FP4X4),
                     rhs_scale=w_scales[:, g, :],
-                    start=(k == 0),
-                    stop=(k == 2),
+                    start=(g == POOLED),
+                    stop=(g == 1),
                 )
-            live[("o", x)] = bank
+
+        def add_with_gpsimd(x):
+            part = work.tile([P, F], F32, name="pre", bufs=3)
+            nc.vector.scalar_tensor_tensor(
+                part[:], wd_row[:], disp_m1[:, x : x + 1], live[("proj", x)][:], op0=ALU.mult, op1=ALU.add
+            )
+            live[("pre", x)] = work.tile([P, F], F32, name="pre_biased", bufs=4)
+            nc.gpsimd.tensor_tensor(live[("pre", x)][:], part[:], b_row[:], op=ALU.add)
 
         def offset(x):
-            term = work.tile([P, F], F32, name="term", bufs=3)
-            nc.vector.scalar_tensor_tensor(term[:], wd_row[:], disp_m1[:, x : x + 1], b_row[:], op0=ALU.mult, op1=ALU.add)
-            live[("t", x)] = term
+            live[("offset", x)] = work.tile([P, F], F32, name="offset", bufs=3)
+            nc.vector.scalar_tensor_tensor(
+                live[("offset", x)][:], wd_row[:], disp_m1[:, x : x + 1], b_row[:], op0=ALU.mult, op1=ALU.add
+            )
 
-        def add(x, cols=slice(0, F)):
+        def add_offset(x, cols):
             if cols.start == 0:
-                live[("p", x)] = work.tile([P, F], F32, name="pre", bufs=3)
-            pre = live[("p", x)]
-            if x not in BIAS_G:
-                nc.vector.tensor_tensor(pre[:, cols], live[("o", x)][:, cols], live[("t", x)][:, cols], op=ALU.add)
-                return
-            nc.vector.scalar_tensor_tensor(pre[:], wd_row[:], disp_m1[:, x : x + 1], live[("o", x)][:], op0=ALU.mult, op1=ALU.add)
-            full = work.tile([P, F], F32, name="full", bufs=3)
-            nc.gpsimd.tensor_tensor(full[:], pre[:], b_row[:], op=ALU.add)
-            live[("p", x)] = full
+                live[("pre", x)] = work.tile([P, F], F32, name="pre", bufs=3)
+            nc.vector.tensor_tensor(
+                live[("pre", x)][:, cols], live[("proj", x)][:, cols], live[("offset", x)][:, cols], op=ALU.add
+            )
 
-        def finish(x, engine, cols=slice(0, F)):
+        def finish(x, cols=slice(0, F), on_vector=False):
             y, n = divmod(x, NT)
             if cols.start == 0:
-                live[("res", x)] = work.tile([P, F], F32, name="res", bufs=4)
-            res = live[("res", x)]
-            if engine == "V":
-                nc.vector.tensor_scalar(res[:, cols], live[("p", x)][:, cols], 0.0, None, op0=ALU.max)
-            elif engine == "G":
-                nc.gpsimd.tensor_scalar(res[:, cols], live[("p", x)][:, cols], 0.0, 0.0, op0=ALU.max, op1=ALU.add)
+                live[("result", x)] = work.tile([P, F], F32, name="result", bufs=4)
+            result = live[("result", x)]
+            if on_vector:
+                nc.vector.tensor_scalar(result[:, cols], live[("pre", x)][:, cols], 0.0, None, op0=ALU.max)
             else:
-                nc.scalar.activation(out=res[:, cols], in_=live[("p", x)][:, cols], func=ACT.Relu)
-            nc.sync.dma_start(out=out[y].rearrange("(q n) f -> q n f", n=NT)[:, n, cols], in_=res[:, cols])
+                nc.scalar.activation(out=result[:, cols], in_=live[("pre", x)][:, cols], func=ACT.Relu)
+            nc.sync.dma_start(out=out[y].rearrange("(q n) f -> q n f", n=NT)[:, n, cols], in_=result[:, cols])
 
-        def turn_terms(h, tags):
-            bank = turn_bank(BF16, tags)
-            for k in range(8):
-                if h == 1:
-                    src = row_terms[:, k, :]
-                else:
-                    x = 4 * h + k
-                    src = col_terms[:, x * TERMS : x * TERMS + P]
-                nc.tensor.transpose(bank[:, k * P : (k + 1) * P], src, ident16[:])
-            live[("terms", h)] = bank
-
-        def empty_terms(h):
-            dst = stationary[:] if h == 1 else moving[:, 4 * h : 4 * h + 8, :]
-            nc.scalar.copy(out=dst.rearrange("p k i -> p (k i)"), in_=live[("terms", h)][:])
-
-
-        for t in range(4):
-            for s in (t, t + 4):
-                for block in range(4):
-                    widen(0, s, block, False)
-                    if small:
-                        small.pop(0)()
-            if t == 2:
-                turn_terms(1, ("expo1",))
-                turn_terms(0, ("expo0",))
-                empty_terms(1)
-                empty_terms(0)
-            turn_right(0, 0, t, (("turn0", "turn1", "corr1", "corr2")[t],))
-            empty(("r", 0, 0, t), True)
-            if t == 1:
-                turn_left(0, ("corr0",))
-                empty(("l", 0), False)
-        centres(0, ("proj",))
-        exponent(0, 0)
-        exponent(0, 1)
-        for k, t in enumerate((0, 2, 1, 3)):
-            flip(2 * t)
-            flip(2 * t + 1)
-            quantise_right(0, 0, k)
-            if k == 1:
-                quantise_left(0)
-        pooled_square(0)
-        window(0, 0)
-        window(0, 1)
-        for t, tag in ((0, "turn0"), (2, "turn1"), (1, "corr2"), (3, "proj")):
-            turn_right(0, 1, t, (tag,))
-            empty(("r", 0, 1, t), False, True)
-            if t == 1:
-                correlate(0, 0)
-                correlate(0, 1)
-        pooled_exp(0)
-        turns.clear()
-        turn_left(1)
-        centres(1)
-        exponent(1, 0)
-        exponent(1, 1)
-        empty(("l", 1), False)
-        for t in range(4):
-            quantise_right(0, 1, t)
-        pooled_square(1)
-        correlate(0, 2)
-        turn_left(2)
-        turn_terms(2, ("turn1",))
-        turns.clear()
-        quantise_left(1)
-        for s in (0, 4):
-            for block in range(4):
-                widen(1, s, block, False)
+        for t in (0, 1):
+            widen(0, t)
+            if t == 0:
+                turn(("centre", 0), "proj")
+                empty(("centre", 0))
+                turn(("left", 0), "corr0")
+            widen(0, t + 4)
+            flip(t)
+            turn(("right", 0, 0, t), TURN_BANKS[t])
+            empty(("right", 0, 0, t))
+        empty(("left", 0))
+        turn(("left", 1), "proj")
+        pooled_window(0)
+        for s in (2, 6, 3):
+            widen(0, s)
+        turn(("tap",), "corr1")
+        turn(("pixel", 0, 4), "corr2")
+        empty(("pixel", 0, 4))
+        empty(("tap",))
+        for s in (5, 4, 2, 3):
+            flip(s)
+        quantise(("right", 0, 0, 0))
+        widen(0, 7)
+        for t in (2, 3):
+            turn(("right", 0, 0, t), TURN_BANKS[t - 2])
+            empty(("right", 0, 0, t))
+        widen(1, 0)
+        widen(1, 4)
+        flip(6)
+        flip(7)
+        for t, bank in ((2, "corr2"), (0, "corr1"), (1, "turn0"), (3, "turn1")):
+            turn(("right", 0, 1, t), bank)
+        for t in (0, 2, 1, 3):
+            empty(("right", 0, 1, t))
+        widen(1, 1)
+        quantise(("right", 0, 0, 1))
+        widen(1, 5)
+        quantise(("left", 0))
+        flip(1)
+        quantise(("right", 0, 0, 2))
+        quantise(("right", 0, 0, 3))
+        for t in (0, 2, 1, 3):
+            quantise(("right", 0, 1, t))
+        flip(0)
+        for g in (0, 1):
+            exponent(0, g)
+            window(0, g)
+        correlate(0, 0)
+        turn(("centre", 1), "turn0")
+        correlate(0, 1)
+        correlate(0, POOLED)
+        empty(("centre", 1))
+        empty(("left", 1))
         begin(0)
+        for g in (0, 1, POOLED):
+            weigh(0, g)
+        exponent(1, 0)
+        turn(("left", 2), "turn1")
+        turn(("pixel", 4, 12), "turn0")
+        exponent(1, 1)
+        window(1, 0)
+        empty(("left", 2))
+        window(1, 1)
+        empty(("pixel", 4, 12))
+        pooled_window(1)
+        quantise_cg(0, 0, 2)
+        quantise(("left", 1))
+        widen(1, 2)
+        quantise_cg(0, POOLED, 3)
+        widen(1, 6)
+        quantise(("left", 2))
+        for g in (POOLED, 0, 1):
+            correlate(1, g)
+        exponent(2, 0)
+        turn(("right", 1, 0, 0), "turn1")
+        turn(("right", 1, 0, 1), "turn0")
+        exponent(2, 1)
+        project(0)
+        begin(1)
 
         jobs = {
-            -1: [("l", 2)],
-            0: [("r", 1, 0, 0), ("r", 1, 0, 1)],
-            1: [("l", 3), ("c", 2)],
-            2: [("r", 1, 0, 2), ("r", 1, 0, 3)],
-            3: [("l", 4), ("c", 3)],
-            4: [("r", 1, 1, 0), ("r", 1, 1, 2)],
-            5: [("r", 1, 1, 1), ("r", 1, 1, 3)],
-            6: [("l", 5), ("c", 4)],
-            7: [("l", 6), ("c", 5)],
-            9: [("l", 7), ("c", 6)],
-            11: [("c", 7)],
+            0: [("right", 1, 0, 0), ("right", 1, 0, 1)],
+            1: [("left", 3), ("centre", 2)],
+            2: [("right", 1, 0, 2), ("right", 1, 0, 3)],
+            3: [("left", 4), ("centre", 3)],
+            4: [("right", 1, 1, 0), ("right", 1, 1, 2)],
+            5: [("right", 1, 1, 1), ("right", 1, 1, 3)],
+            6: [("left", 5), ("centre", 4)],
+            7: [("left", 6), ("centre", 5)],
+            8: [("pixel", 12, 16)],
+            9: [("left", 7), ("centre", 6)],
+            11: [("centre", 7)],
         }
-        exps = {0: 1, 3: 2, 5: 3, 7: 4, 9: 5, 11: 6, 13: 7}
-        flips = {1: (0, 1), 2: (4, 5), 3: (2, 3), 4: (6, 7)}
-
-        for x in range(TILES + 1):
-            if x >= 2:
-                add(x - 2)
-            if x >= 1:
-                project(x - 1)
-            for job in jobs.get(x - 1, []):
-                if job[0] != "c":
-                    empty(job, job[0] == "r" and job[2] == 0)
-            if x == 0:
-                empty_terms(2)
-            if x + 1 < TILES:
+        flips = {2: (4, 5), 3: (2, 3), 4: (6, 7)}
+        turned = 1
+        for x in range(1, TILES):
+            arrived = jobs.get(x - 1, [])
+            for job in arrived:
+                if job[0] != "centre":
+                    empty(job)
+            if x < LAST:
                 window(x + 1, 0)
                 window(x + 1, 1)
-            for job in jobs.get(x - 1, []):
-                if job[0] == "c":
-                    pooled_square(job[1])
-            if x in exps:
-                pooled_exp(exps[x])
-            for g in (0, 1, 2) if x % NT == 0 else (2, 0, 1):
-                if x < TILES:
-                    weigh(x, g)
-                if x + 1 < TILES:
+            for job in arrived:
+                if job[0] == "centre":
+                    empty(job)
+            if x % 2 == 1 and 1 < x < LAST:
+                pooled_window((x + 1) // 2)
+            for g in (0, 1, POOLED) if x == NT else (POOLED, 0, 1):
+                weigh(x, g)
+                if x < LAST:
                     correlate(x + 1, g)
-            if x >= 3:
-                finish(x - 3, "V" if x - 3 in RELU_V else "S")
-            if x < 3:
-                for s in (x + 1, x + 5):
-                    for block in range(4):
-                        widen(1, s, block, block < WIDEN_S1)
+            if x >= 2:
+                finish(x - 2)
+            if x == 2:
+                widen(1, 3)
+                widen(1, 7)
             for s in flips.get(x, ()):
                 flip(s)
-            for job in jobs.get(x - 1, []):
-                if job[0] == "l":
-                    quantise_left(job[1])
-                elif job[0] == "r":
-                    quantise_right(job[1], job[2], job[3])
+            for job in arrived:
+                if job[0] in ("left", "right"):
+                    quantise(job)
             for job in jobs.get(x, []):
-                if job[0] == "l":
-                    turn_left(job[1])
-                elif job[0] == "c":
-                    centres(job[1])
-                else:
-                    turn_right(job[1], job[2], job[3])
+                turn(job, TURN_BANKS[turned % 2])
+                turned += 1
             if x + 2 < TILES:
                 exponent(x + 2, 0)
                 exponent(x + 2, 1)
-            if x - 1 not in BIAS_G and 1 <= x:
-                offset(x - 1)
-            if x < TILES:
-                quantise_cg(x, 2, 3)
+            if x < LAST:
+                quantise_cg(x, POOLED, 3)
+                if x == LAST - 2:
+                    offset(LAST - 1)
+                add_with_gpsimd(x - 1)
                 quantise_cg(x, 0, 2)
-            if x + 1 < TILES:
+                project(x)
                 begin(x + 1)
-        last = TILES - 1
-        add(last, slice(0, F // 2))
-        add(last, slice(F // 2, F))
-        finish(last - 1, "S")
-        finish(last, "S", slice(0, F // 2))
-        finish(last, "V", slice(F // 2, F))
+
+        for g in (POOLED, 0, 1):
+            quantise_cg(LAST, g, g + 1)
+            project(LAST, (g,))
+        offset(LAST)
+        add_offset(LAST - 1, slice(0, F))
+        add_offset(LAST, slice(0, F // 2))
+        add_offset(LAST, slice(F // 2, F))
+        finish(LAST, slice(0, F // 2))
+        finish(LAST, slice(F // 2, F), on_vector=True)
+        finish(LAST - 1)

import math
from contextlib import ExitStack

import concourse.mybir as mybir
from concourse.masks import make_identity

H, W, D, F = 2, 1024, 512, 512
L = W + W // 2
FLOPS = 2 * H * W * W * D + 2 * H * W * L * F

F32 = mybir.dt.float32
BF16 = mybir.dt.bfloat16
I32 = mybir.dt.int32
U32 = mybir.dt.uint32
U8 = mybir.dt.uint8
FP8 = mybir.dt.float8_e4m3fn
FP8X4 = mybir.dt.float8_e4m3fn_x4
FP4X4 = mybir.dt.float4_e2m1fn_x4
ALU = mybir.AluOpType
ACT = mybir.ActivationFunctionType
AXIS_X = mybir.AxisListType.X

P = 128
NT = W // P
TILES = H * NT
LAST = TILES - 1
POOLED = 2
TERMS = 16
ORIGIN = 512
TWO_VAR = 128.0 * 128.0
DISP_LIMIT = 1024.0
LN_RANGE = 2.0**64
TURN_BANKS = ("turn0", "turn1")


def tile_stereocorrpyramidmotionencoder_d2p_kernel(
    tc, f_left, f_right_bytes, f_right_scale, disp, gain, w_corr_words, w_corr_scales, w_disp, b_mot, out
):
    nc = tc.nc
    with ExitStack() as ctx:
        keep = ctx.enter_context(tc.tile_pool(name="keep", bufs=1))
        work = ctx.enter_context(tc.tile_pool(name="work", bufs=2))
        psum = ctx.enter_context(tc.psum_pool(name="psum", bufs=1))
        ctx.enter_context(tc.manual_schedule())

        def kept(name, shape, dtype):
            return keep.tile(shape, dtype, name=name, align_bytes=64)

        scale_all = kept("scale_all", [P, H * 8 * 4], F32)
        gain_rows = kept("gain_rows", [P, NT], BF16)
        gain_k = kept("gain_k", [P, 3, 4], BF16)
        disp_i = kept("disp_i", [P, H, NT], BF16)
        right_bytes = [kept("right_bytes%d" % y, [P, NT, D], U8) for y in range(H)]
        left = [kept("left%d" % y, [P, NT, D], BF16) for y in range(H)]
        wd_row = kept("wd_row", [P, F], BF16)
        b_row = kept("b_row", [P, F], BF16)
        w_words = kept("w_words", [P, 3, 2 * F], U8)
        w_scales = kept("w_scales", [P, 3, F], U8)

        nc.sync.dma_start(out=scale_all[:], in_=f_right_scale.rearrange("y j d -> (y j d)").partition_broadcast(P))
        nc.sync.dma_start(out=gain_rows[:], in_=gain[0:W].rearrange("(m s) -> m s", s=NT))
        nc.scalar.dma_start(out=gain_k[:], in_=gain.rearrange("(g p t) -> p g t", p=P, t=4))
        nc.scalar.dma_start(out=disp_i[:], in_=disp.rearrange("y (q n) -> q y n", n=NT))

        def load_right(y, half):
            src = f_right_bytes[y].rearrange("(m a b c) d -> m a b (c d)", a=2, b=2, c=2)
            dst = right_bytes[y][:].rearrange("m (a b c) d -> m a b (c d)", a=2, b=2)
            nc.sync.dma_start(out=dst[:, :, half, :], in_=src[:, :, half, :])

        def load_left(y, n0, n1):
            src = f_left[y].rearrange("(q n) d -> q n d", n=NT)
            nc.sync.dma_start(out=left[y][:, n0:n1, :], in_=src[:, n0:n1, :])

        nc.vector.memset(w_scales[:].rearrange("p g n -> p (g n)").bitcast(I32), 0)
        load_right(0, 0)
        load_right(0, 1)
        for n0 in (0, 2, 4):
            load_left(0, n0, n0 + 2)
        load_right(1, 0)
        for quadrant in range(4):
            nc.sync.dma_start(
                out=w_scales[32 * quadrant : 32 * quadrant + 4, :, :].bitcast(I32),
                in_=w_corr_scales[:, 4 * quadrant : 4 * quadrant + 4, :].rearrange("g r n -> r g n").bitcast(I32),
            )
        nc.sync.dma_start(out=w_words[:].bitcast(I32), in_=w_corr_words.rearrange("g p n -> p g n").bitcast(I32))
        nc.sync.dma_start(out=wd_row[:], in_=w_disp.partition_broadcast(P))
        nc.sync.dma_start(out=b_row[:], in_=b_mot.partition_broadcast(P))
        load_right(1, 1)
        load_left(0, 6, 8)
        load_left(1, 0, 4)
        load_left(1, 4, 8)

        def counted(name, pattern, step):
            tile = kept(name, [P] + [count for (stride, count) in pattern], F32)
            nc.gpsimd.iota(tile[:], pattern, base=-ORIGIN, channel_multiplier=step, allow_small_or_imprecise_dtypes=True)
            return tile[:].rearrange("p a b -> p (a b)")

        ident32 = kept("ident32", [P, P], F32)
        make_identity(nc, ident32[:])
        pixel = counted("pixel", [[0, H], [1, NT]], 8)
        tap = counted("tap", [[512, 2], [1, 4]], 4)
        ident16 = kept("ident16", [P, P], BF16)
        pixel_high = pixel[:, 0:1]

        pixel_terms = kept("pixel_terms", [P, TILES * TERMS + P - TERMS], BF16)
        tap_terms = kept("tap_terms", [P, 8, P], BF16)
        pixel_v = pixel_terms[:, 0 : TILES * TERMS].rearrange("p (x k) -> p x k", k=TERMS)
        tap_v = tap_terms[:].rearrange("p (g t) k -> p g t k", t=4)
        pick = kept("pick", [P, 8], F32)
        half_tap2 = kept("half_tap2", [P, 8], F32)
        pooled_pos = kept("pooled_pos", [P, 4], F32)
        nc.vector.memset(pixel_terms[:], 0.0)
        nc.vector.memset(tap_terms[:], 0.0)
        nc.vector.tensor_reduce(pick[:], ident32[:].rearrange("p (b r) -> p b r", r=16), axis=AXIS_X, op=ALU.add)
        nc.vector.memset(tap_terms[:, :, 6:9], 1.0)
        nc.vector.memset(pixel_v[:, :, 9:12], 1.0)
        nc.vector.tensor_copy(out=ident16[:], in_=ident32[:])
        nc.vector.tensor_copy(out=pixel_v[:, :, 0:6:3], in_=pixel_high.unsqueeze(2).to_broadcast([P, TILES, 2]))
        nc.vector.tensor_scalar(
            pixel_v[:, :, 1:6:3], pixel.unsqueeze(2).to_broadcast([P, TILES, 2]), pixel_high, None, op0=ALU.subtract
        )
        for g in range(2):
            nc.vector.tensor_copy(
                out=tap_v[:, g, :, 0:3], in_=tap[:, 4 * g : 4 * g + 1].unsqueeze(2).to_broadcast([P, 4, 3])
            )
            nc.vector.tensor_scalar(
                tap_v[:, g, :, 3:6], pixel[:, 0:4].unsqueeze(2).to_broadcast([P, 4, 3]), pixel_high, None, op0=ALU.subtract
            )
        nc.vector.scalar_tensor_tensor(half_tap2[:], tap, -0.5, tap, op0=ALU.mult, op1=ALU.mult)
        nc.vector.tensor_scalar(pooled_pos[:], tap[:, 4:8], 1.0 / 128.0, (0.5 - ORIGIN) / 256.0, op0=ALU.mult, op1=ALU.add)

        picked = kept("picked", [P, H, 4, 8], F32)
        scale_m = kept("scale_m", [P, H * 4], F32)
        half_sign = kept("half_sign", [P, NT], F32)
        half_sign_pooled = kept("half_sign_pooled", [P, 4], F32)
        scale_signed = kept("scale_signed", [P, H, NT, 4], F32)
        resign = kept("resign", [P, 4, 2], F32)
        gain_abs = kept("gain_abs", [P, 12], F32)
        factors = kept("factors", [P, 3, 12], F32)
        logs = kept("logs", [P, 3, 12], F32)
        log_gain = kept("log_gain", [P, 12], F32)
        low_part = kept("low_part", [P, 12], F32)
        disp_clamped = kept("disp_clamped", [P, TILES], F32)
        disp_m1 = kept("disp_m1", [P, TILES], F32)
        centre = kept("centre", [P, TILES], F32)
        whole = kept("whole", [P, TILES + 8], F32)
        rest1 = kept("rest1", [P, TILES + 8], F32)
        rest2 = kept("rest2", [P, TILES + 8], F32)
        pieces = kept("pieces", [P, 3, TILES + 8], BF16)
        one = kept("one", [P, 1], F32)
        gain_flat = gain_k[:].rearrange("p g t -> p (g t)")
        disp_flat = disp_i[:].rearrange("p y n -> p (y n)")

        def sign_scales(y):
            nc.vector.scalar_tensor_tensor(
                scale_signed[:, y, :, :],
                scale_m[:, 4 * y : 4 * y + 4].unsqueeze(1).to_broadcast([P, NT, 4]),
                2.0,
                half_sign[:].unsqueeze(2).to_broadcast([P, NT, 4]),
                op0=ALU.mult,
                op1=ALU.mult,
            )

        nc.vector.tensor_tensor(
            picked[:],
            scale_all[:].rearrange("p (y b d) -> p y d b", y=H, d=4),
            pick[:].unsqueeze(1).unsqueeze(1).to_broadcast([P, H, 4, 8]),
            op=ALU.mult,
        )
        nc.vector.tensor_scalar(half_sign[:], gain_rows[:], 0.0, 0.5, op0=ALU.is_ge, op1=ALU.subtract)
        nc.vector.scalar_tensor_tensor(gain_abs[:], gain_flat, -1.0, gain_flat, op0=ALU.mult, op1=ALU.max)
        nc.vector.tensor_reduce(scale_m[:], picked[:].rearrange("p y d b -> p (y d) b"), axis=AXIS_X, op=ALU.add)
        nc.vector.tensor_scalar(low_part[:], gain_abs[:], 1.0 / LN_RANGE, LN_RANGE, op0=ALU.min, op1=ALU.mult)
        nc.vector.tensor_scalar(factors[:, 0, :], gain_abs[:], 1.0 / LN_RANGE, LN_RANGE, op0=ALU.max, op1=ALU.min)
        sign_scales(0)
        nc.vector.tensor_scalar(factors[:, 1, :], gain_abs[:], 1.0 / LN_RANGE, 1.0, op0=ALU.mult, op1=ALU.max)
        nc.vector.tensor_scalar(factors[:, 2, :], low_part[:], 1.0 / LN_RANGE, None, op0=ALU.max)
        nc.scalar.activation(out=logs[:], in_=factors[:], func=ACT.Ln)
        nc.scalar.activation(out=one[:], in_=logs[:, 0, 0:1], func=ACT.Exp, scale=0.0)

        between = [
            lambda: nc.vector.tensor_scalar(disp_clamped[:], disp_flat, DISP_LIMIT, -DISP_LIMIT, op0=ALU.min, op1=ALU.max),
            lambda: nc.vector.tensor_scalar(half_sign_pooled[:], gain_k[:, POOLED, :], 0.0, 0.5, op0=ALU.is_ge, op1=ALU.subtract),
            lambda: nc.vector.scalar_tensor_tensor(centre[:], disp_clamped[:], -128.0, pixel, op0=ALU.mult, op1=ALU.add),
            lambda: nc.vector.scalar_tensor_tensor(
                resign[:],
                half_sign[:].rearrange("p (t e) -> p t e", e=2),
                4.0,
                half_sign_pooled[:].unsqueeze(2).to_broadcast([P, 4, 2]),
                op0=ALU.mult,
                op1=ALU.mult,
            ),
            lambda: nc.vector.tensor_scalar(
                pixel_v[:, :, 2:6:3], disp_clamped[:].unsqueeze(2).to_broadcast([P, TILES, 2]), -128.0, None, op0=ALU.mult
            ),
            lambda: nc.vector.scalar_tensor_tensor(whole[:, 0:TILES], centre[:], -0.5, centre[:], op0=ALU.mult, op1=ALU.mult),
            lambda: nc.vector.tensor_reduce(log_gain[:], logs[:].rearrange("p r k -> p k r"), axis=AXIS_X, op=ALU.add),
            None,
            lambda: nc.vector.scalar_tensor_tensor(
                whole[:, TILES:], log_gain[:, 0:8], TWO_VAR, half_tap2[:], op0=ALU.mult, op1=ALU.add
            ),
            lambda: sign_scales(1),
            lambda: nc.vector.tensor_copy(out=pieces[:, 0, :], in_=whole[:]),
            None,
            lambda: nc.vector.tensor_tensor(rest1[:], whole[:], pieces[:, 0, :], op=ALU.subtract),
            None,
            lambda: nc.vector.tensor_copy(out=pieces[:, 1, :], in_=rest1[:]),
            None,
            lambda: nc.vector.tensor_tensor(rest2[:], rest1[:], pieces[:, 1, :], op=ALU.subtract),
            None,
            lambda: nc.vector.tensor_copy(out=pieces[:, 2, :], in_=rest2[:]),
            None,
            lambda: nc.vector.tensor_copy(out=tap_terms[:, :, 9:12], in_=pieces[:, :, TILES:].rearrange("p r x -> p x r")),
            lambda: nc.vector.tensor_copy(out=pixel_v[:, :, 6:9], in_=pieces[:, :, 0:TILES].rearrange("p r x -> p x r")),
            lambda: nc.vector.tensor_scalar(disp_m1[:], disp_flat, one[:], None, op0=ALU.subtract),
        ]

        right_rows = [kept("right_rows%d" % level, [P, NT, D], BF16) for level in range(2)]
        r_codes = [[kept("r_codes%d%d" % (y, level), [P, 4, 256], U32) for level in range(2)] for y in range(H)]
        r_scales = [[kept("r_scales%d%d" % (y, level), [P, 4, 256], U8) for level in range(2)] for y in range(H)]
        l_codes = [kept("l_codes%d" % y, [P, W], U32) for y in range(H)]
        l_scales = [kept("l_scales%d" % y, [P, W], U8) for y in range(H)]
        moving = kept("moving", [P, TILES, P], BF16)
        stationary = kept("stationary", [P, 8, P], BF16)
        live = {}

        def bank_tile(shape, dtype, bank):
            return psum.tile(shape, dtype, name=bank, tag=bank)

        def widen(y, s):
            rows = right_rows[0][:, s, :].rearrange("p (u w e) -> p w u e", u=2, e=2)
            for block in range(4):
                src = right_bytes[y][:, s, block * P : (block + 1) * P].bitcast(FP8)
                nc.vector.tensor_scalar(
                    rows[:, block * 32 : (block + 1) * 32, :, :],
                    src.rearrange("p (w u e) -> p w u e", u=2, e=2),
                    scale_signed[:, y, s, block : block + 1],
                    None,
                    op0=ALU.mult,
                )
                step = between.pop(0) if between else None
                if step:
                    step()

        def flip(s):
            nc.vector.tensor_scalar(
                right_rows[1][:, s, :], right_rows[0][:, s, :], resign[:, s // 2, s % 2 : s % 2 + 1], None, op0=ALU.mult
            )

        def turn(job, bank):
            if job[0] in ("pixel", "tap"):
                tile = bank_tile([P, 8 * P], BF16, bank)
                if job[0] == "tap":
                    sources = [tap_terms[:, k, :] for k in range(8)]
                else:
                    sources = [pixel_terms[:, x * TERMS : x * TERMS + P] for x in range(job[1], job[2])]
                identity = ident16
            else:
                tile = bank_tile([P, 4 * P], F32, bank)
                identity = ident32
                if job[0] == "centre":
                    sources = [centre[:, x : x + 1].to_broadcast([P, P]) for x in (2 * job[1], 2 * job[1] + 1)]
                elif job[0] == "left":
                    y, n = divmod(2 * job[1], NT)
                    sources = [left[y][:, n + a, :].bitcast(F32)[:, u:256:2] for a in range(2) for u in range(2)]
                else:
                    level, t = job[2:]
                    rows = (2 * t, 2 * t + 1) if level else (t, t + 4)
                    sources = [right_rows[level][:, s, :].bitcast(F32)[:, u * P : (u + 1) * P] for s in rows for u in range(2)]
            for k, source in enumerate(sources):
                nc.tensor.transpose(tile[:, k * P : (k + 1) * P], source, identity[:])
            live[job] = tile

        def empty(job):
            tile = live[job]
            if job[0] == "tap":
                nc.scalar.copy(out=stationary[:].rearrange("p k i -> p (k i)"), in_=tile[:])
            elif job[0] == "pixel":
                nc.scalar.copy(
                    out=moving[:, job[1] : job[2], :].rearrange("p k i -> p (k i)"), in_=tile[:, 0 : (job[2] - job[1]) * P]
                )
            elif job[0] == "centre":
                squares = work.tile([P, 4, 2 * P], F32, name="pooled_win", bufs=3)
                for t in range(4):
                    nc.scalar.activation(
                        out=squares[:, t, :],
                        in_=tile[:, 0 : 2 * P],
                        func=ACT.Square,
                        scale=-1.0 / 256.0,
                        bias=pooled_pos[:, t : t + 1],
                    )
                live[("pooled_win", job[1])] = squares
            else:
                grouped = work.tile([P, 4 * P], F32, name="grouped", bufs=8, align_bytes=64)
                if job[0] == "right" and job[2] == 0:
                    nc.scalar.copy(
                        out=grouped[:].rearrange("p (m a) -> p m a", a=4), in_=tile[:].rearrange("p (a m) -> p m a", a=4)
                    )
                else:
                    nc.scalar.copy(
                        out=grouped[:].rearrange("p (e m u) -> p e m u", e=2, u=2),
                        in_=tile[:].rearrange("p (e u m) -> p e m u", e=2, u=2),
                    )
                live[job] = grouped

        def quantise(job):
            if job[0] == "left":
                y, n = divmod(2 * job[1], NT)
                codes, scales = l_codes[y][:, n * P : (n + 2) * P], l_scales[y][:, n * P : (n + 2) * P]
            else:
                y, level, t = job[1:]
                codes, scales = r_codes[y][level][:, t, :], r_scales[y][level][:, t, :]
            nc.vector.quantize_mx(out=codes.bitcast(FP8X4), scales=scales, in_=live[job][:].bitcast(BF16))

        def pooled_window(pair):
            win = live[("pooled_win", pair)]
            for t in range(4):
                nc.scalar.activation(
                    out=win[:, t, :], in_=win[:, t, :], func=ACT.Exp, scale=-0.5, bias=log_gain[:, 8 + t : 9 + t]
                )

        def exponent(x, g):
            tile = bank_tile([P, 4, P], F32, "expo%d" % g)
            for t in range(4):
                nc.tensor.matmul(tile[:, t, :], lhsT=stationary[:, 4 * g + t, :], rhs=moving[:, x, :], start=True, stop=True)
            live[("expo", x, g)] = tile

        def window(x, g):
            win = work.tile([P, P, 4], F32, name="win", bufs=8)
            nc.scalar.activation(
                out=win[:], in_=live[("expo", x, g)][:].rearrange("p t q -> p q t"), func=ACT.Exp, scale=1.0 / TWO_VAR
            )
            live[("win", x, g)] = win

        def correlate(x, g):
            y, n = divmod(x, NT)
            cols = slice(n * P, (n + 1) * P)
            level = g // POOLED
            halves = (0, 1) if level else (g,)
            tile = bank_tile([P, 4, P], F32, "corr%d" % g)
            for t in range(4):
                for e in halves:
                    nc.tensor.matmul_mx(
                        out=tile[:, t, :],
                        lhsT=r_codes[y][level][:, t, e * P : (e + 1) * P].bitcast(FP8X4),
                        lhsT_scale=r_scales[y][level][:, t, e * P : (e + 1) * P],
                        rhs=l_codes[y][:, cols].bitcast(FP8X4),
                        rhs_scale=l_scales[y][:, cols],
                        start=(e == halves[0]),
                        stop=(e == halves[-1]),
                    )
            live[("corr", x, g)] = tile

        def begin(x):
            live[("cg", x)] = work.tile([P, 3, 4 * P], BF16, name="cg", bufs=4, align_bytes=64)
            live[("cg_codes", x)] = work.tile([P, 3, P], U32, name="cg_codes", bufs=4, align_bytes=64)
            live[("cg_scales", x)] = work.tile([P, 3, P], U8, name="cg_scales", bufs=4, align_bytes=64)

        def weigh(x, g):
            if g == POOLED:
                first = (x % 2) * P
                win = live[("pooled_win", x // 2)][:, :, first : first + P].rearrange("p t q -> p q t")
            else:
                win = live[("win", x, g)][:]
            nc.vector.scalar_tensor_tensor(
                live[("cg", x)][:, g, :].rearrange("p (q t) -> p q t", t=4),
                live[("corr", x, g)][:].rearrange("p t q -> p q t"),
                (0.5 if g == POOLED else 1.0) / math.sqrt(D),
                win,
                op0=ALU.mult,
                op1=ALU.mult,
            )

        def quantise_cg(x, g0, g1):
            nc.vector.quantize_mx(
                out=live[("cg_codes", x)][:, g0:g1, :].rearrange("p g q -> p (g q)").bitcast(FP8X4),
                scales=live[("cg_scales", x)][:, g0:g1, :].rearrange("p g q -> p (g q)"),
                in_=live[("cg", x)][:, g0:g1, :].rearrange("p g c -> p (g c)"),
            )

        def project(x, passes=(POOLED, 0, 1)):
            if passes[0] == POOLED:
                live[("proj", x)] = bank_tile([P, F], F32, "expo0" if x == LAST else "proj")
            for g in passes:
                nc.tensor.matmul_mx(
                    out=live[("proj", x)][:],
                    lhsT=live[("cg_codes", x)][:, g, :].bitcast(FP8X4),
                    lhsT_scale=live[("cg_scales", x)][:, g, :],
                    rhs=w_words[:, g, :].bitcast(FP4X4),
                    rhs_scale=w_scales[:, g, :],
                    start=(g == POOLED),
                    stop=(g == 1),
                )

        def add_with_gpsimd(x):
            part = work.tile([P, F], F32, name="pre", bufs=3)
            nc.vector.scalar_tensor_tensor(
                part[:], wd_row[:], disp_m1[:, x : x + 1], live[("proj", x)][:], op0=ALU.mult, op1=ALU.add
            )
            live[("pre", x)] = work.tile([P, F], F32, name="pre_biased", bufs=4)
            nc.gpsimd.tensor_tensor(live[("pre", x)][:], part[:], b_row[:], op=ALU.add)

        def offset(x):
            live[("offset", x)] = work.tile([P, F], F32, name="offset", bufs=3)
            nc.vector.scalar_tensor_tensor(
                live[("offset", x)][:], wd_row[:], disp_m1[:, x : x + 1], b_row[:], op0=ALU.mult, op1=ALU.add
            )

        def add_offset(x, cols):
            if cols.start == 0:
                live[("pre", x)] = work.tile([P, F], F32, name="pre", bufs=3)
            nc.vector.tensor_tensor(
                live[("pre", x)][:, cols], live[("proj", x)][:, cols], live[("offset", x)][:, cols], op=ALU.add
            )

        def finish(x, cols=slice(0, F), on_vector=False):
            y, n = divmod(x, NT)
            if cols.start == 0:
                live[("result", x)] = work.tile([P, F], F32, name="result", bufs=4)
            result = live[("result", x)]
            if on_vector:
                nc.vector.tensor_scalar(result[:, cols], live[("pre", x)][:, cols], 0.0, None, op0=ALU.max)
            else:
                nc.scalar.activation(out=result[:, cols], in_=live[("pre", x)][:, cols], func=ACT.Relu)
            nc.sync.dma_start(out=out[y].rearrange("(q n) f -> q n f", n=NT)[:, n, cols], in_=result[:, cols])

        for t in (0, 1):
            widen(0, t)
            if t == 0:
                turn(("centre", 0), "proj")
                empty(("centre", 0))
                turn(("left", 0), "corr0")
            widen(0, t + 4)
            flip(t)
            turn(("right", 0, 0, t), TURN_BANKS[t])
            empty(("right", 0, 0, t))
        empty(("left", 0))
        turn(("left", 1), "proj")
        pooled_window(0)
        for s in (2, 6, 3):
            widen(0, s)
        turn(("tap",), "corr1")
        turn(("pixel", 0, 4), "corr2")
        empty(("pixel", 0, 4))
        empty(("tap",))
        for s in (5, 4, 2, 3):
            flip(s)
        quantise(("right", 0, 0, 0))
        widen(0, 7)
        for t in (2, 3):
            turn(("right", 0, 0, t), TURN_BANKS[t - 2])
            empty(("right", 0, 0, t))
        widen(1, 0)
        widen(1, 4)
        flip(6)
        flip(7)
        for t, bank in ((2, "corr2"), (0, "corr1"), (1, "turn0"), (3, "turn1")):
            turn(("right", 0, 1, t), bank)
        for t in (0, 2, 1, 3):
            empty(("right", 0, 1, t))
        widen(1, 1)
        quantise(("right", 0, 0, 1))
        widen(1, 5)
        quantise(("left", 0))
        flip(1)
        quantise(("right", 0, 0, 2))
        quantise(("right", 0, 0, 3))
        for t in (0, 2, 1, 3):
            quantise(("right", 0, 1, t))
        flip(0)
        for g in (0, 1):
            exponent(0, g)
            window(0, g)
        correlate(0, 0)
        turn(("centre", 1), "turn0")
        correlate(0, 1)
        correlate(0, POOLED)
        empty(("centre", 1))
        empty(("left", 1))
        begin(0)
        for g in (0, 1, POOLED):
            weigh(0, g)
        exponent(1, 0)
        turn(("left", 2), "turn1")
        turn(("pixel", 4, 12), "turn0")
        exponent(1, 1)
        window(1, 0)
        empty(("left", 2))
        window(1, 1)
        empty(("pixel", 4, 12))
        pooled_window(1)
        quantise_cg(0, 0, 2)
        quantise(("left", 1))
        widen(1, 2)
        quantise_cg(0, POOLED, 3)
        widen(1, 6)
        quantise(("left", 2))
        for g in (POOLED, 0, 1):
            correlate(1, g)
        exponent(2, 0)
        turn(("right", 1, 0, 0), "turn1")
        turn(("right", 1, 0, 1), "turn0")
        exponent(2, 1)
        project(0)
        begin(1)

        jobs = {
            0: [("right", 1, 0, 0), ("right", 1, 0, 1)],
            1: [("left", 3), ("centre", 2)],
            2: [("right", 1, 0, 2), ("right", 1, 0, 3)],
            3: [("left", 4), ("centre", 3)],
            4: [("right", 1, 1, 0), ("right", 1, 1, 2)],
            5: [("right", 1, 1, 1), ("right", 1, 1, 3)],
            6: [("left", 5), ("centre", 4)],
            7: [("left", 6), ("centre", 5)],
            8: [("pixel", 12, 16)],
            9: [("left", 7), ("centre", 6)],
            11: [("centre", 7)],
        }
        flips = {2: (4, 5), 3: (2, 3), 4: (6, 7)}
        turned = 1
        for x in range(1, TILES):
            arrived = jobs.get(x - 1, [])
            for job in arrived:
                if job[0] != "centre":
                    empty(job)
            if x < LAST:
                window(x + 1, 0)
                window(x + 1, 1)
            for job in arrived:
                if job[0] == "centre":
                    empty(job)
            if x % 2 == 1 and 1 < x < LAST:
                pooled_window((x + 1) // 2)
            for g in (0, 1, POOLED) if x == NT else (POOLED, 0, 1):
                weigh(x, g)
                if x < LAST:
                    correlate(x + 1, g)
            if x >= 2:
                finish(x - 2)
            if x == 2:
                widen(1, 3)
                widen(1, 7)
            for s in flips.get(x, ()):
                flip(s)
            for job in arrived:
                if job[0] in ("left", "right"):
                    quantise(job)
            for job in jobs.get(x, []):
                turn(job, TURN_BANKS[turned % 2])
                turned += 1
            if x + 2 < TILES:
                exponent(x + 2, 0)
                exponent(x + 2, 1)
            if x < LAST:
                quantise_cg(x, POOLED, 3)
                if x == LAST - 2:
                    offset(LAST - 1)
                add_with_gpsimd(x - 1)
                quantise_cg(x, 0, 2)
                project(x)
                begin(x + 1)

        for g in (POOLED, 0, 1):
            quantise_cg(LAST, g, g + 1)
            project(LAST, (g,))
        offset(LAST)
        add_offset(LAST - 1, slice(0, F))
        add_offset(LAST, slice(0, F // 2))
        add_offset(LAST, slice(F // 2, F))
        finish(LAST, slice(0, F // 2))
        finish(LAST, slice(F // 2, F), on_vector=True)
        finish(LAST - 1)
